import numpy as np
import ml_dtypes


def mxq(x, axis, fmt="e4m3"):
    dtype, down = {"e4m3": (ml_dtypes.float8_e4m3fn, 7), "e5m2": (ml_dtypes.float8_e5m2, 14)}[fmt]
    v = np.moveaxis(np.asarray(x, np.float32).astype(ml_dtypes.bfloat16).astype(np.float64), axis, -1)
    blocks = v.reshape(v.shape[:-1] + (-1, 32))
    amax = np.abs(blocks).max(-1, keepdims=True)
    byte = np.maximum(np.where(amax > 0, np.frexp(amax)[1] - 1 + 127, 0) - down, 1)
    scale = np.exp2(byte - 127.0)
    codes = (blocks / scale).astype(np.float32).astype(dtype).astype(np.float64)
    return np.moveaxis((codes * scale).reshape(v.shape), -1, axis)


WIDE = False


def mx_kscale(k):
    if not WIDE:
        return np.ones(k)
    levels = np.array([10, -10, 5, -5, 0])
    if k % 512:
        return np.exp2(np.random.permutation(np.resize(levels, k // 32))).repeat(32)
    a = np.empty((k // 512, 16))
    for p in range(k // 512):
        a[p, :8] = np.random.permutation(np.resize(levels, 8))
        for g in range(8):
            far = levels[np.abs(levels - a[p, g]) >= 10]
            a[p, g + 8] = far[np.random.randint(len(far))]
    return np.exp2(a.ravel()).repeat(32)


def f64(x):
    return np.asarray(x).astype(np.float64)


def striped(idx):
    return np.tile(idx.reshape(-1, 16).T, (8, 1)).astype(np.uint16)


def unstriped(offs):
    return offs[:16].T.reshape(-1).astype(np.int64)


E2M1 = np.array([0.0, 0.5, 1.0, 1.5, 2.0, 3.0, 4.0, 6.0, -0.0, -0.5, -1.0, -1.5, -2.0, -3.0, -4.0, -6.0])


def pack_weight(w, fmt):
    k, n = w.shape
    w = f64(np.asarray(w, np.float32).astype(ml_dtypes.bfloat16)).reshape(k // 32, 32, n)
    amax = np.abs(w).max(1)
    if fmt == "e4m3":
        byte = np.frexp(amax)[1] - 1 + 127 - 7
    else:
        mant, ex = np.frexp(amax / 6.0)
        byte = np.where(mant > 0.5, ex, ex - 1) + 127
    byte = np.clip(np.where(amax > 0, byte, 1), 1, 254)
    scaled = (w * np.exp2(127.0 - byte)[:, None, :]).reshape(k, n).astype(np.float32)
    by_word = np.ascontiguousarray(scaled.reshape(k // 512, 128, 4, n).transpose(0, 1, 3, 2))
    if fmt == "e4m3":
        words = by_word.astype(ml_dtypes.float8_e4m3fn).view(np.uint8)
    else:
        c = by_word.astype(ml_dtypes.float4_e2m1fn).view(np.uint8) & 0xF
        words = (c[..., 0::2] | (c[..., 1::2] << 4)).reshape(k // 512, 128, 2 * n)
    return np.ascontiguousarray(words), np.ascontiguousarray(byte.astype(np.uint8).reshape(k // 512, 16, n))


def unpack_weight(words, scales, fmt):
    g, _, n = scales.shape
    words = np.ascontiguousarray(words).reshape(g, 128, n, -1)
    if fmt == "e4m3":
        vals = words.view(ml_dtypes.float8_e4m3fn).astype(np.float64)
    else:
        nib = np.empty((g, 128, n, 4), np.uint8)
        nib[..., 0::2] = words & 0xF
        nib[..., 1::2] = words >> 4
        vals = E2M1[nib]
    vals = vals * np.repeat(np.exp2(scales.astype(np.float64) - 127.0), 8, axis=1)[..., None]
    return vals.transpose(0, 1, 3, 2).reshape(g * 512, n)


def sigmoid(v):
    return 1.0 / (1.0 + np.exp(-np.maximum(v, -700.0)))


K, T, E, C, H, N = 512, 512, 6, 256, 512, 128
TOP = 3


def by_expert(wq, xq):
    return np.concatenate([wq[e].T @ xq[:, e * C:(e + 1) * C] for e in range(E)], axis=1)


def setup_inputs():
    n = np.random.standard_normal
    s = mx_kscale(K)[:, None]
    u = mx_kscale(H)
    deal = np.repeat(np.arange(E), C).reshape(TOP, T)[:, np.random.permutation(T)]
    deal = np.take_along_axis(deal, np.argsort(np.random.rand(TOP, T), axis=0), axis=0)
    for _ in range(8):
        s_, t_ = np.random.permutation(T).reshape(2, -1); r = np.random.randint(TOP, size=T // 2); x, y = deal[r, s_].copy(), deal[r, t_].copy()
        ok = ~((deal[:, s_] == y).any(0) | (deal[:, t_] == x).any(0)); deal[r[ok], s_[ok]] = y[ok]; deal[r[ok], t_[ok]] = x[ok]
    order = np.lexsort((np.random.rand(TOP * T), deal.reshape(-1)))
    slot_token = order % T; pos = np.empty(TOP * T, np.int64); pos[order] = np.arange(TOP * T); pos = pos.reshape(TOP, T)
    g = np.random.uniform(0.5, 1.5, (TOP, T)); g = g / g.sum(0)
    w1 = [pack_weight(m, "e2m1") for m in n((E, K, H)) / np.sqrt(K) / s[None]]
    w3 = [pack_weight(m, "e2m1") for m in n((E, K, H)) / np.sqrt(K) / s[None] * u[None, None, :]]
    w2 = [pack_weight(m, "e2m1") for m in n((E, H, N)) / np.sqrt(H) / u[None, :, None]]
    return {
        "xT": (n((K, T)) * s).astype(np.float32),
        "w1_words": np.stack([m[0] for m in w1]),
        "w1_scales": np.stack([m[1] for m in w1]),
        "w3_words": np.stack([m[0] for m in w3]),
        "w3_scales": np.stack([m[1] for m in w3]),
        "w2_words": np.stack([m[0] for m in w2]),
        "w2_scales": np.stack([m[1] for m in w2]),
        "gate": np.stack([np.tile(r, (N, 1)) for r in g]).astype(np.float32),
        "offs": striped(slot_token),
        "pos1": striped(pos[0]),
        "pos2": striped(pos[1]),
        "pos3": striped(pos[2]),
    }


def reference(xT, w1_words, w1_scales, w3_words, w3_scales, w2_words, w2_scales, gate, offs, pos1, pos2, pos3):
    idx = unstriped(offs)
    w1 = np.stack([unpack_weight(w1_words[e], w1_scales[e], "e2m1") for e in range(E)])
    w3 = np.stack([unpack_weight(w3_words[e], w3_scales[e], "e2m1") for e in range(E)])
    w2 = np.stack([unpack_weight(w2_words[e], w2_scales[e], "e2m1") for e in range(E)])
    xq = mxq(f64(xT)[:, idx], 0, "e4m3")
    h = sigmoid(by_expert(w1, xq))
    h = h * by_expert(w3, xq)
    y = by_expert(w2, mxq(h, 0, "e4m3"))
    return sum(f64(gate[r]) * y[:, unstriped(p)] for r, p in enumerate((pos1, pos2, pos3)))

@@ -1,0 +1,215 @@
+from contextlib import ExitStack
+
+import concourse.mybir as mybir
+from concourse.masks import make_identity
+
+P = 128
+K, T, E, C, H, N = 512, 512, 6, 256, 512, 128
+S = E * C
+TOP = 3
+FLOPS = 2 * S * (2 * K * H + H * N)
+
+F32 = mybir.dt.float32
+BF16 = mybir.dt.bfloat16
+I32 = mybir.dt.int32
+U32 = mybir.dt.uint32
+U16 = mybir.dt.uint16
+U8 = mybir.dt.uint8
+FP8X4 = mybir.dt.float8_e4m3fn_x4
+FP4X4 = mybir.dt.float4_e2m1fn_x4
+SIGMOID = mybir.ActivationFunctionType.Sigmoid
+MULT = mybir.AluOpType.mult
+ADD = mybir.AluOpType.add
+
+
+def tile_moe_tk_glu_sigmoid_kernel(
+    tc, xT, w1_words, w1_scales, w3_words, w3_scales, w2_words, w2_scales, gate, offs, pos1, pos2, pos3, out
+):
+    nc = tc.nc
+    with ExitStack() as ctx:
+        keep = ctx.enter_context(tc.tile_pool(name="keep", bufs=1))
+        work = ctx.enter_context(tc.tile_pool(name="work", bufs=6))
+        psum = ctx.enter_context(tc.psum_pool(name="psum", bufs=2))
+
+        warm = keep.tile([P, 1], F32, name="warm")
+        nc.vector.memset(warm[:], 0.0)
+        warm2 = keep.tile([P, 1], F32, name="warm2")
+        nc.scalar.activation(warm2[:], warm[:], SIGMOID)
+
+        x_view = xT.rearrange("(p j) t -> p j t", j=4)
+        x_raw = []
+        offs_t = keep.tile([P, S // 16], U16, name="offs_t")
+        nc.sync.dma_start(offs_t[:], offs)
+        x_cuts = [(0, 256), (256, 384), (384, 512)]
+        for c, (t0, t1) in enumerate(x_cuts):
+            xr = keep.tile([P, 4, t1 - t0], F32, name=f"x_raw{c}")
+            nc.sync.dma_start(out=xr[:], in_=x_view[:, :, t0:t1])
+            x_raw.append(xr)
+
+        sc1 = keep.tile([P, E * H], U8, align_bytes=64, name="sc1")
+        sc3 = keep.tile([P, E * H], U8, align_bytes=64, name="sc3")
+        sc2 = keep.tile([P, E * N], U8, align_bytes=64, name="sc2")
+        xs = keep.tile([P, T], U8, align_bytes=64, name="xs")
+        nc.vector.memset(sc1[:].bitcast(I32), 0)
+        nc.vector.memset(sc3[:].bitcast(I32), 0)
+        nc.vector.memset(sc2[:].bitcast(I32), 0)
+        nc.vector.memset(xs[:].bitcast(I32), 0)
+
+        def load_words(words, width, e0, e1, name, eng):
+            t = keep.tile([P, (e1 - e0) * 2 * width], U8, align_bytes=64, name=name)
+            src = words.bitcast(I32)[e0:e1, 0].rearrange("e p c -> p e c")
+            eng.dma_start(out=t[:].bitcast(I32).rearrange("p (e c) -> p e c", e=e1 - e0), in_=src)
+            return [t[:, i * 2 * width : (i + 1) * 2 * width] for i in range(e1 - e0)]
+
+        def load_scales(tile, scales, eng):
+            src = scales.bitcast(I32)
+            for q in range(4):
+                eng.dma_start(
+                    out=tile[:].bitcast(I32)[32 * q : 32 * q + 4, :].rearrange("p (e c) -> p e c", e=E),
+                    in_=src[:, 0, 4 * q : 4 * q + 4, :].rearrange("e q c -> q e c"),
+                )
+
+        ident = keep.tile([P, P], F32, name="ident")
+        make_identity(nc, ident[:])
+        w1 = load_words(w1_words, H, 0, 1, "w1_a", nc.gpsimd)
+        w3 = load_words(w3_words, H, 0, 1, "w3_a", nc.gpsimd)
+        load_scales(sc1, w1_scales, nc.sync)
+        load_scales(sc3, w3_scales, nc.sync)
+        load_scales(sc2, w2_scales, nc.sync)
+        w1 += load_words(w1_words, H, 1, 3, "w1_b", nc.gpsimd)
+        w3 += load_words(w3_words, H, 1, 3, "w3_b", nc.gpsimd)
+        w2 = load_words(w2_words, N, 0, E, "w2_t", nc.gpsimd)
+        w1 += load_words(w1_words, H, 3, 6, "w1_c", nc.sync)
+        w3 += load_words(w3_words, H, 3, 6, "w3_c", nc.sync)
+        pos_t = []
+        for r, pos in enumerate((pos1, pos2, pos3)):
+            pt = keep.tile([P, T // 16], U16, name=f"pos_t{r}")
+            nc.sync.dma_start(pt[:], pos)
+            pos_t.append(pt)
+        gate_t = keep.tile([P, TOP, T], F32, name="gate_t")
+        nc.sync.dma_start(out=gate_t[:], in_=gate.rearrange("r p t -> p r t"))
+
+        xw = keep.tile([P, T], U32, align_bytes=64, name="xw")
+        for c, (t0, t1) in enumerate(x_cuts):
+            xb = keep.tile([P, t1 - t0, 4], BF16, align_bytes=64, name=f"x_bf{c}")
+            (nc.scalar.copy if c == 2 else nc.vector.tensor_copy)(out=xb[:], in_=x_raw[c][:].rearrange("p j t -> p t j"))
+            cols = slice(t0, t1)
+            nc.vector.quantize_mx(
+                out=xw[:, cols].bitcast(FP8X4), scales=xs[:, cols], in_=xb[:].rearrange("p t j -> p (t j)")
+            )
+
+        y_all = keep.tile([P, S], F32, name="y_all")
+        gw = {}
+        gs = {}
+        h_bf = {}
+        ht_ps = {}
+
+        def gather(e, pieces):
+            a = work.tile([P, C], U32, align_bytes=64, name="gw_t", bufs=3)
+            b = work.tile([P, C], U8, align_bytes=64, name="gs_t", bufs=3)
+            n = C // pieces
+            for i in range(pieces):
+                idx = offs_t[:, (e * C + i * n) // 16 : (e * C + (i + 1) * n) // 16]
+                nc.vector.tensor_copy(a[:, i * n : (i + 1) * n], xw[:].indirect(idx))
+                nc.vector.tensor_copy(b[:, i * n : (i + 1) * n], xs[:].indirect(idx))
+            gw[e] = a
+            gs[e] = b
+
+        sigs = {}
+
+        def product(e, s, w, sc, nm):
+            cols = slice(s * P, (s + 1) * P)
+            ps = psum.tile([P, H], F32, name=nm)
+            nc.tensor.matmul_mx(
+                out=ps[:],
+                lhsT=gw[e][:, cols].bitcast(FP8X4),
+                lhsT_scale=gs[e][:, cols],
+                rhs=w[e].bitcast(FP4X4),
+                rhs_scale=sc[:, e * H : (e + 1) * H],
+                start=True,
+                stop=True,
+            )
+            return ps
+
+        def first_a(e, s):
+            ps = product(e, s, w1, sc1, "a_ps")
+            sig = work.tile([P, H], F32, name="sig")
+            nc.scalar.activation(sig[:], ps[:], SIGMOID)
+            sigs[e, s] = sig
+
+        def first_b(e, s):
+            ps = product(e, s, w3, sc3, "b_ps")
+            sig = sigs[e, s]
+            h = work.tile([P, H], BF16, align_bytes=64, name="h_bf")
+            turned = "p (m u d) -> p u m d"
+            nc.vector.tensor_tensor(
+                h[:].rearrange("p (u m d) -> p u m d", u=2, d=2),
+                ps[:].rearrange(turned, u=2, d=2),
+                sig[:].rearrange(turned, u=2, d=2),
+                MULT,
+            )
+            h_bf[e, s] = h
+
+        def turn(e, tiles):
+            n = len(tiles) * P
+            ps = psum.tile([P, 2, n], F32, name="ht_ps")
+            for i, s in enumerate(tiles):
+                words = h_bf[e, s][:].bitcast(F32)
+                for u in range(2):
+                    nc.tensor.transpose(ps[:, u, i * P : (i + 1) * P], words[:, u * P : (u + 1) * P], ident[:])
+            ht_ps[e, tiles[0]] = ps
+
+        flats = {}
+
+        def lift(e, tiles):
+            n = len(tiles) * P
+            ht = work.tile([P, n, 4], BF16, align_bytes=64, name="ht")
+            flat = ht[:].rearrange("p r d -> p (r d)")
+            flats[e, tiles[0]] = flat
+            nc.scalar.copy(
+                flat.bitcast(F32).rearrange("p (r u) -> p r u", u=2), ht_ps[e, tiles[0]][:].rearrange("p u r -> p r u")
+            )
+
+        def second(e, tiles):
+            n = len(tiles) * P
+            c0 = e * C + tiles[0] * P
+            flat = flats[e, tiles[0]]
+            hw = work.tile([P, n], U32, align_bytes=64, name="hw")
+            hs = work.tile([P, n], U8, align_bytes=64, name="hs")
+            nc.vector.quantize_mx(out=hw[:].bitcast(FP8X4), scales=hs[:], in_=flat)
+            yp = psum.tile([P, n], F32, name="y_ps")
+            nc.tensor.matmul_mx(
+                out=yp[:],
+                lhsT=w2[e].bitcast(FP4X4),
+                lhsT_scale=sc2[:, e * N : (e + 1) * N],
+                rhs=hw[:].bitcast(FP8X4),
+                rhs_scale=hs[:],
+                start=True,
+                stop=True,
+            )
+            nc.scalar.copy(y_all[:, c0 : c0 + n], yp[:])
+
+        for e in range(E):
+            gather(e, 2 if e == 0 else 1)
+            first_a(e, 0)
+            first_a(e, 1)
+            for tiles in ([0], [1]) if e >= 3 else ([0, 1],):
+                for s in tiles:
+                    first_b(e, s)
+                turn(e, tiles)
+                lift(e, tiles)
+                second(e, tiles)
+
+        terms = []
+        for r in range(TOP):
+            t = keep.tile([P, T], F32, name=f"term{r}")
+            nc.vector.tensor_tensor(t[:], y_all[:].indirect(pos_t[r][:]), gate_t[:, r, :], MULT)
+            terms.append(t)
+        halves = [slice(0, T // 2), slice(T // 2, T)]
+        part = keep.tile([P, T], F32, name="part")
+        res = keep.tile([P, T], F32, name="res")
+        for hf in halves:
+            nc.vector.tensor_tensor(part[:, hf], terms[0][:, hf], terms[1][:, hf], ADD)
+        for hf in halves:
+            nc.vector.tensor_tensor(res[:, hf], part[:, hf], terms[2][:, hf], ADD)
+            nc.sync.dma_start(out=out[:, hf], in_=res[:, hf])

@@ -7,6 +7,8 @@ P = 128
 K, T, E, C, H, N = 512, 512, 6, 256, 512, 128
 S = E * C
 TOP = 3
+FINE = 2
+LAG = 3
 FLOPS = 2 * S * (2 * K * H + H * N)
 
 F32 = mybir.dt.float32
@@ -28,32 +30,30 @@ def tile_moe_tk_glu_sigmoid_kernel(
     nc = tc.nc
     with ExitStack() as ctx:
         keep = ctx.enter_context(tc.tile_pool(name="keep", bufs=1))
-        work = ctx.enter_context(tc.tile_pool(name="work", bufs=6))
-        psum = ctx.enter_context(tc.psum_pool(name="psum", bufs=2))
+        work = ctx.enter_context(tc.tile_pool(name="work", bufs=3))
+        psum = ctx.enter_context(tc.psum_pool(name="psum", bufs=1))
 
         warm = keep.tile([P, 1], F32, name="warm")
         nc.vector.memset(warm[:], 0.0)
         warm2 = keep.tile([P, 1], F32, name="warm2")
         nc.scalar.activation(warm2[:], warm[:], SIGMOID)
 
-        x_view = xT.rearrange("(p j) t -> p j t", j=4)
-        x_raw = []
-        offs_t = keep.tile([P, S // 16], U16, name="offs_t")
-        nc.sync.dma_start(offs_t[:], offs)
-        x_cuts = [(0, 256), (256, 384), (384, 512)]
-        for c, (t0, t1) in enumerate(x_cuts):
-            xr = keep.tile([P, 4, t1 - t0], F32, name=f"x_raw{c}")
-            nc.sync.dma_start(out=xr[:], in_=x_view[:, :, t0:t1])
-            x_raw.append(xr)
-
         sc1 = keep.tile([P, E * H], U8, align_bytes=64, name="sc1")
         sc3 = keep.tile([P, E * H], U8, align_bytes=64, name="sc3")
         sc2 = keep.tile([P, E * N], U8, align_bytes=64, name="sc2")
         xs = keep.tile([P, T], U8, align_bytes=64, name="xs")
         nc.vector.memset(sc1[:].bitcast(I32), 0)
+        nc.vector.memset(xs[:].bitcast(I32), 0)
         nc.vector.memset(sc3[:].bitcast(I32), 0)
         nc.vector.memset(sc2[:].bitcast(I32), 0)
-        nc.vector.memset(xs[:].bitcast(I32), 0)
+
+        x_view = xT.rearrange("(p j) t -> p j t", j=4)
+        x_raw = []
+        x_cuts = [(0, 256), (256, 384), (384, 512)]
+        for c, (t0, t1) in enumerate(x_cuts):
+            xr = keep.tile([P, 4, t1 - t0], F32, name=f"x_raw{c}")
+            nc.sync.dma_start(out=xr[:], in_=x_view[:, :, t0:t1])
+            x_raw.append(xr)
 
         def load_words(words, width, e0, e1, name, eng):
             t = keep.tile([P, (e1 - e0) * 2 * width], U8, align_bytes=64, name=name)
@@ -71,16 +71,17 @@ def tile_moe_tk_glu_sigmoid_kernel(
 
         ident = keep.tile([P, P], F32, name="ident")
         make_identity(nc, ident[:])
-        w1 = load_words(w1_words, H, 0, 1, "w1_a", nc.gpsimd)
-        w3 = load_words(w3_words, H, 0, 1, "w3_a", nc.gpsimd)
+        offs_t = keep.tile([P, S // 16], U16, name="offs_t")
+        nc.sync.dma_start(offs_t[:], offs)
+        w1 = load_words(w1_words, H, 0, 1, "w1_a", nc.sync)
         load_scales(sc1, w1_scales, nc.sync)
+        w1 += load_words(w1_words, H, 1, 4, "w1_b", nc.sync)
         load_scales(sc3, w3_scales, nc.sync)
+        w3 = load_words(w3_words, H, 0, 2, "w3_a", nc.sync)
+        w1 += load_words(w1_words, H, 4, 6, "w1_c", nc.sync)
+        w3 += load_words(w3_words, H, 2, 6, "w3_b", nc.sync)
+        w2 = load_words(w2_words, N, 0, E, "w2_t", nc.sync)
         load_scales(sc2, w2_scales, nc.sync)
-        w1 += load_words(w1_words, H, 1, 3, "w1_b", nc.gpsimd)
-        w3 += load_words(w3_words, H, 1, 3, "w3_b", nc.gpsimd)
-        w2 = load_words(w2_words, N, 0, E, "w2_t", nc.gpsimd)
-        w1 += load_words(w1_words, H, 3, 6, "w1_c", nc.sync)
-        w3 += load_words(w3_words, H, 3, 6, "w3_c", nc.sync)
         pos_t = []
         for r, pos in enumerate((pos1, pos2, pos3)):
             pt = keep.tile([P, T // 16], U16, name=f"pos_t{r}")
@@ -92,94 +93,92 @@ def tile_moe_tk_glu_sigmoid_kernel(
         xw = keep.tile([P, T], U32, align_bytes=64, name="xw")
         for c, (t0, t1) in enumerate(x_cuts):
             xb = keep.tile([P, t1 - t0, 4], BF16, align_bytes=64, name=f"x_bf{c}")
-            (nc.scalar.copy if c == 2 else nc.vector.tensor_copy)(out=xb[:], in_=x_raw[c][:].rearrange("p j t -> p t j"))
+            (nc.scalar.copy if c == 1 else nc.vector.tensor_copy)(out=xb[:], in_=x_raw[c][:].rearrange("p j t -> p t j"))
             cols = slice(t0, t1)
             nc.vector.quantize_mx(
                 out=xw[:, cols].bitcast(FP8X4), scales=xs[:, cols], in_=xb[:].rearrange("p t j -> p (t j)")
             )
 
         y_all = keep.tile([P, S], F32, name="y_all")
-        gw = {}
-        gs = {}
-        h_bf = {}
-        ht_ps = {}
+        gw = []
+        gs = []
+        for g, n_tiles in enumerate([1, 1, 2, 2, 2, 2, 2]):
+            n = n_tiles * P
+            a = keep.tile([P, n], U32, align_bytes=64, name=f"gw{g}")
+            b = keep.tile([P, n], U8, align_bytes=64, name=f"gs{g}")
+            c0 = len(gw) * P // 16
+            idx = offs_t[:, c0 : c0 + n // 16]
+            nc.vector.tensor_copy(a[:], xw[:].indirect(idx))
+            nc.vector.tensor_copy(b[:], xs[:].indirect(idx))
+            for i in range(n_tiles):
+                gw.append(a[:, i * P : (i + 1) * P])
+                gs.append(b[:, i * P : (i + 1) * P])
 
-        def gather(e, pieces):
-            a = work.tile([P, C], U32, align_bytes=64, name="gw_t", bufs=3)
-            b = work.tile([P, C], U8, align_bytes=64, name="gs_t", bufs=3)
-            n = C // pieces
-            for i in range(pieces):
-                idx = offs_t[:, (e * C + i * n) // 16 : (e * C + (i + 1) * n) // 16]
-                nc.vector.tensor_copy(a[:, i * n : (i + 1) * n], xw[:].indirect(idx))
-                nc.vector.tensor_copy(b[:, i * n : (i + 1) * n], xs[:].indirect(idx))
-            gw[e] = a
-            gs[e] = b
+        banks = [psum.tile([P, H], F32, name=f"bank{b}") for b in range(8)]
 
-        sigs = {}
-
-        def product(e, s, w, sc, nm):
-            cols = slice(s * P, (s + 1) * P)
-            ps = psum.tile([P, H], F32, name=nm)
+        def product(i, w, sc, bank):
+            e = i // 2
             nc.tensor.matmul_mx(
-                out=ps[:],
-                lhsT=gw[e][:, cols].bitcast(FP8X4),
-                lhsT_scale=gs[e][:, cols],
+                out=bank[:],
+                lhsT=gw[i].bitcast(FP8X4),
+                lhsT_scale=gs[i],
                 rhs=w[e].bitcast(FP4X4),
                 rhs_scale=sc[:, e * H : (e + 1) * H],
                 start=True,
                 stop=True,
             )
-            return ps
 
-        def first_a(e, s):
-            ps = product(e, s, w1, sc1, "a_ps")
-            sig = work.tile([P, H], F32, name="sig")
-            nc.scalar.activation(sig[:], ps[:], SIGMOID)
-            sigs[e, s] = sig
+        read = "p (m u d) -> p u m d"
+        laid = "p (u m d) -> p u m d"
+        sigs = []
+        for i in range(S // P):
+            bank = banks[2 + i if i < 2 else 4 + (i - 2) % 4]
+            product(i, w1, sc1, bank)
+            sig = keep.tile([P, H], F32, name=f"sig{i}")
+            nc.scalar.activation(sig[:].rearrange(laid, u=2, d=2), bank[:].rearrange(read, u=2, d=2), SIGMOID)
+            sigs.append(sig)
 
-        def first_b(e, s):
-            ps = product(e, s, w3, sc3, "b_ps")
-            sig = sigs[e, s]
-            h = work.tile([P, H], BF16, align_bytes=64, name="h_bf")
-            turned = "p (m u d) -> p u m d"
+        def b_bank(i):
+            return banks[(1, 3, 4, 5)[i // 2 % 4] if i % 2 else (0, 2)[i // 2 % 2]]
+
+        def linear(e):
+            for i in (2 * e, 2 * e + 1):
+                product(i, w3, sc3, b_bank(i))
+
+        h_bf = {}
+
+        def gated(i):
+            h = keep.tile([P, H], BF16, align_bytes=64, name=f"h_bf{i}")
             nc.vector.tensor_tensor(
-                h[:].rearrange("p (u m d) -> p u m d", u=2, d=2),
-                ps[:].rearrange(turned, u=2, d=2),
-                sig[:].rearrange(turned, u=2, d=2),
+                h[:].rearrange(laid, u=2, d=2),
+                b_bank(i)[:].rearrange(read, u=2, d=2),
+                sigs[i][:].rearrange(laid, u=2, d=2),
                 MULT,
             )
-            h_bf[e, s] = h
+            h_bf[i] = h
 
-        def turn(e, tiles):
+        def turn(tiles):
             n = len(tiles) * P
-            ps = psum.tile([P, 2, n], F32, name="ht_ps")
-            for i, s in enumerate(tiles):
-                words = h_bf[e, s][:].bitcast(F32)
+            tp = b_bank(tiles[-1])[:, : 2 * n].rearrange("p (u r) -> p u r", u=2)
+            for k, i in enumerate(tiles):
+                words = h_bf[i][:].bitcast(F32)
                 for u in range(2):
-                    nc.tensor.transpose(ps[:, u, i * P : (i + 1) * P], words[:, u * P : (u + 1) * P], ident[:])
-            ht_ps[e, tiles[0]] = ps
-
-        flats = {}
-
-        def lift(e, tiles):
-            n = len(tiles) * P
-            ht = work.tile([P, n, 4], BF16, align_bytes=64, name="ht")
+                    nc.tensor.transpose(tp[:, u, k * P : (k + 1) * P], words[:, u * P : (u + 1) * P], ident[:])
+            ht = keep.tile([P, n, 4], BF16, align_bytes=64, name=f"ht{tiles[0]}")
             flat = ht[:].rearrange("p r d -> p (r d)")
-            flats[e, tiles[0]] = flat
-            nc.scalar.copy(
-                flat.bitcast(F32).rearrange("p (r u) -> p r u", u=2), ht_ps[e, tiles[0]][:].rearrange("p u r -> p r u")
-            )
+            nc.scalar.copy(flat.bitcast(F32).rearrange("p (r u) -> p r u", u=2), tp.rearrange("p u r -> p r u"))
+            return flat
 
-        def second(e, tiles):
+        def second(k, tiles, flat):
             n = len(tiles) * P
-            c0 = e * C + tiles[0] * P
-            flat = flats[e, tiles[0]]
-            hw = work.tile([P, n], U32, align_bytes=64, name="hw")
-            hs = work.tile([P, n], U8, align_bytes=64, name="hs")
+            c0 = tiles[0] * P
+            e = tiles[0] // 2
+            hw = keep.tile([P, n], U32, align_bytes=64, name=f"hw{k}")
+            hs = keep.tile([P, n], U8, align_bytes=64, name=f"hs{k}")
             nc.vector.quantize_mx(out=hw[:].bitcast(FP8X4), scales=hs[:], in_=flat)
-            yp = psum.tile([P, n], F32, name="y_ps")
+            yp = banks[6 + k % 2][:, :n]
             nc.tensor.matmul_mx(
-                out=yp[:],
+                out=yp,
                 lhsT=w2[e].bitcast(FP4X4),
                 lhsT_scale=sc2[:, e * N : (e + 1) * N],
                 rhs=hw[:].bitcast(FP8X4),
@@ -187,29 +186,33 @@ def tile_moe_tk_glu_sigmoid_kernel(
                 start=True,
                 stop=True,
             )
-            nc.scalar.copy(y_all[:, c0 : c0 + n], yp[:])
+            nc.scalar.copy(y_all[:, c0 : c0 + n], yp)
 
-        for e in range(E):
-            gather(e, 2 if e == 0 else 1)
-            first_a(e, 0)
-            first_a(e, 1)
-            for tiles in ([0], [1]) if e >= 3 else ([0, 1],):
-                for s in tiles:
-                    first_b(e, s)
-                turn(e, tiles)
-                lift(e, tiles)
-                second(e, tiles)
+        units = [[2 * e, 2 * e + 1] for e in range(E - FINE)] + [[i] for i in range(2 * (E - FINE), 2 * E)]
+        linear(0)
+        waiting = []
+        for k, tiles in enumerate(units):
+            for i in tiles:
+                gated(i)
+            if tiles[-1] % 2 and tiles[-1] + 1 < 2 * E:
+                linear(tiles[-1] // 2 + 1)
+            waiting.append((k, tiles, turn(tiles)))
+            if len(waiting) > LAG:
+                second(*waiting.pop(0))
+        for job in waiting:
+            second(*job)
 
-        terms = []
-        for r in range(TOP):
-            t = keep.tile([P, T], F32, name=f"term{r}")
-            nc.vector.tensor_tensor(t[:], y_all[:].indirect(pos_t[r][:]), gate_t[:, r, :], MULT)
-            terms.append(t)
-        halves = [slice(0, T // 2), slice(T // 2, T)]
-        part = keep.tile([P, T], F32, name="part")
-        res = keep.tile([P, T], F32, name="res")
-        for hf in halves:
-            nc.vector.tensor_tensor(part[:, hf], terms[0][:, hf], terms[1][:, hf], ADD)
-        for hf in halves:
-            nc.vector.tensor_tensor(res[:, hf], part[:, hf], terms[2][:, hf], ADD)
-            nc.sync.dma_start(out=out[:, hf], in_=res[:, hf])
+        for c, (t0, t1) in enumerate([(0, 256), (256, 512)]):
+            n = t1 - t0
+            terms = []
+            for r in range(TOP):
+                t = keep.tile([P, n], F32, name=f"term{c}_{r}")
+                nc.vector.tensor_tensor(
+                    t[:], y_all[:].indirect(pos_t[r][:, t0 // 16 : t1 // 16]), gate_t[:, r, t0:t1], MULT
+                )
+                terms.append(t)
+            part = keep.tile([P, n], F32, name=f"part{c}")
+            res = keep.tile([P, n], F32, name=f"res{c}")
+            nc.vector.tensor_tensor(part[:], terms[0][:], terms[1][:], ADD)
+            nc.vector.tensor_tensor(res[:], part[:], terms[2][:], ADD)
+            nc.sync.dma_start(out=out[:, t0:t1], in_=res[:])

@@ -7,8 +7,8 @@ P = 128
 K, T, E, C, H, N = 512, 512, 6, 256, 512, 128
 S = E * C
 TOP = 3
-FINE = 2
-LAG = 3
+CUT = 384
+ONV = (4, 6)
 FLOPS = 2 * S * (2 * K * H + H * N)
 
 F32 = mybir.dt.float32
@@ -77,9 +77,9 @@ def tile_moe_tk_glu_sigmoid_kernel(
         load_scales(sc1, w1_scales, nc.sync)
         w1 += load_words(w1_words, H, 1, 4, "w1_b", nc.sync)
         load_scales(sc3, w3_scales, nc.sync)
-        w3 = load_words(w3_words, H, 0, 2, "w3_a", nc.sync)
+        w3 = load_words(w3_words, H, 0, 3, "w3_a", nc.sync)
         w1 += load_words(w1_words, H, 4, 6, "w1_c", nc.sync)
-        w3 += load_words(w3_words, H, 2, 6, "w3_b", nc.sync)
+        w3 += load_words(w3_words, H, 3, 6, "w3_b", nc.sync)
         w2 = load_words(w2_words, N, 0, E, "w2_t", nc.sync)
         load_scales(sc2, w2_scales, nc.sync)
         pos_t = []
@@ -130,55 +130,62 @@ def tile_moe_tk_glu_sigmoid_kernel(
 
         read = "p (m u d) -> p u m d"
         laid = "p (u m d) -> p u m d"
-        sigs = []
-        for i in range(S // P):
-            bank = banks[2 + i if i < 2 else 4 + (i - 2) % 4]
+        sigs = {}
+        h_bf = {}
+        flats = {}
+
+        def gating(i):
+            bank = banks[i if i < 8 else i - 4]
             product(i, w1, sc1, bank)
             sig = keep.tile([P, H], F32, name=f"sig{i}")
             nc.scalar.activation(sig[:].rearrange(laid, u=2, d=2), bank[:].rearrange(read, u=2, d=2), SIGMOID)
-            sigs.append(sig)
+            sigs[i] = sig
 
         def b_bank(i):
-            return banks[(1, 3, 4, 5)[i // 2 % 4] if i % 2 else (0, 2)[i // 2 % 2]]
+            return banks[(1, 3, 1, 4, 5, 7)[i // 2] if i % 2 else (0, 2)[i // 2 % 2]]
 
         def linear(e):
             for i in (2 * e, 2 * e + 1):
                 product(i, w3, sc3, b_bank(i))
 
-        h_bf = {}
-
         def gated(i):
             h = keep.tile([P, H], BF16, align_bytes=64, name=f"h_bf{i}")
-            nc.vector.tensor_tensor(
-                h[:].rearrange(laid, u=2, d=2),
-                b_bank(i)[:].rearrange(read, u=2, d=2),
-                sigs[i][:].rearrange(laid, u=2, d=2),
-                MULT,
-            )
             h_bf[i] = h
+            b = b_bank(i)[:].rearrange(read, u=2, d=2)
+            if i < 2:
+                lin = keep.tile([P, H], F32, name=f"lin{i}")
+                nc.scalar.copy(lin[:].rearrange(laid, u=2, d=2), b)
+                nc.gpsimd.tensor_tensor(h[:], lin[:], sigs[i][:], MULT)
+            else:
+                nc.vector.tensor_tensor(h[:].rearrange(laid, u=2, d=2), b, sigs[i][:].rearrange(laid, u=2, d=2), MULT)
 
-        def turn(tiles):
+        units = [[2 * e, 2 * e + 1] for e in range(E - 1)] + [[2 * E - 2], [2 * E - 1]]
+
+        def t_bank(k):
+            return b_bank(units[k][-1]) if k else banks[6]
+
+        def turn(k):
+            tiles = units[k]
             n = len(tiles) * P
-            tp = b_bank(tiles[-1])[:, : 2 * n].rearrange("p (u r) -> p u r", u=2)
-            for k, i in enumerate(tiles):
+            tp = t_bank(k)[:, : 2 * n].rearrange("p (u r) -> p u r", u=2)
+            for j, i in enumerate(tiles):
                 words = h_bf[i][:].bitcast(F32)
                 for u in range(2):
-                    nc.tensor.transpose(tp[:, u, k * P : (k + 1) * P], words[:, u * P : (u + 1) * P], ident[:])
-            ht = keep.tile([P, n, 4], BF16, align_bytes=64, name=f"ht{tiles[0]}")
+                    nc.tensor.transpose(tp[:, u, j * P : (j + 1) * P], words[:, u * P : (u + 1) * P], ident[:])
+            ht = keep.tile([P, n, 4], BF16, align_bytes=64, name=f"ht{k}")
             flat = ht[:].rearrange("p r d -> p (r d)")
             nc.scalar.copy(flat.bitcast(F32).rearrange("p (r u) -> p r u", u=2), tp.rearrange("p u r -> p r u"))
-            return flat
+            flats[k] = flat
 
-        def second(k, tiles, flat):
+        def second(k):
+            tiles = units[k]
             n = len(tiles) * P
-            c0 = tiles[0] * P
             e = tiles[0] // 2
             hw = keep.tile([P, n], U32, align_bytes=64, name=f"hw{k}")
             hs = keep.tile([P, n], U8, align_bytes=64, name=f"hs{k}")
-            nc.vector.quantize_mx(out=hw[:].bitcast(FP8X4), scales=hs[:], in_=flat)
-            yp = banks[6 + k % 2][:, :n]
+            nc.vector.quantize_mx(out=hw[:].bitcast(FP8X4), scales=hs[:], in_=flats[k])
             nc.tensor.matmul_mx(
-                out=yp,
+                out=t_bank(k)[:, :n],
                 lhsT=w2[e].bitcast(FP4X4),
                 lhsT_scale=sc2[:, e * N : (e + 1) * N],
                 rhs=hw[:].bitcast(FP8X4),
@@ -186,23 +193,41 @@ def tile_moe_tk_glu_sigmoid_kernel(
                 start=True,
                 stop=True,
             )
-            nc.scalar.copy(y_all[:, c0 : c0 + n], yp)
 
-        units = [[2 * e, 2 * e + 1] for e in range(E - FINE)] + [[i] for i in range(2 * (E - FINE), 2 * E)]
+        def fetch(k, copy):
+            c0 = units[k][0] * P
+            n = len(units[k]) * P
+            copy(y_all[:, c0 : c0 + n], t_bank(k)[:, :n])
+
+        for i in range(8):
+            gating(i)
         linear(0)
-        waiting = []
-        for k, tiles in enumerate(units):
-            for i in tiles:
-                gated(i)
-            if tiles[-1] % 2 and tiles[-1] + 1 < 2 * E:
-                linear(tiles[-1] // 2 + 1)
-            waiting.append((k, tiles, turn(tiles)))
-            if len(waiting) > LAG:
-                second(*waiting.pop(0))
-        for job in waiting:
-            second(*job)
+        linear(1)
+        gated(0)
+        gated(1)
+        gating(8)
+        gating(9)
+        linear(2)
+        gating(10)
+        gating(11)
+        for e in range(1, E - 1):
+            gated(2 * e)
+            if e + 2 < E:
+                linear(e + 2)
+            gated(2 * e + 1)
+            turn(e)
+            if e == 2:
+                turn(0)
+        for k in (E - 1, E):
+            gated(units[k][0])
+            turn(k)
+        order = [1, 2, 0, 3, 4, 5, 6]
+        for k in order:
+            second(k)
+        for k in order:
+            fetch(k, nc.vector.tensor_copy if k in ONV else nc.scalar.copy)
 
-        for c, (t0, t1) in enumerate([(0, 256), (256, 512)]):
+        for c, (t0, t1) in enumerate([(0, CUT), (CUT, T)]):
             n = t1 - t0
             terms = []
             for r in range(TOP):

@@ -7,8 +7,9 @@ P = 128
 K, T, E, C, H, N = 512, 512, 6, 256, 512, 128
 S = E * C
 TOP = 3
-CUT = 384
-ONV = (4, 6)
+HELPED = 3
+CUT = 256
+ONV = (4, 5, 6)
 FLOPS = 2 * S * (2 * K * H + H * N)
 
 F32 = mybir.dt.float32
@@ -32,11 +33,6 @@ def tile_moe_tk_glu_sigmoid_kernel(
         keep = ctx.enter_context(tc.tile_pool(name="keep", bufs=1))
         work = ctx.enter_context(tc.tile_pool(name="work", bufs=3))
         psum = ctx.enter_context(tc.psum_pool(name="psum", bufs=1))
-
-        warm = keep.tile([P, 1], F32, name="warm")
-        nc.vector.memset(warm[:], 0.0)
-        warm2 = keep.tile([P, 1], F32, name="warm2")
-        nc.scalar.activation(warm2[:], warm[:], SIGMOID)
 
         sc1 = keep.tile([P, E * H], U8, align_bytes=64, name="sc1")
         sc3 = keep.tile([P, E * H], U8, align_bytes=64, name="sc3")
@@ -77,9 +73,8 @@ def tile_moe_tk_glu_sigmoid_kernel(
         load_scales(sc1, w1_scales, nc.sync)
         w1 += load_words(w1_words, H, 1, 4, "w1_b", nc.sync)
         load_scales(sc3, w3_scales, nc.sync)
-        w3 = load_words(w3_words, H, 0, 3, "w3_a", nc.sync)
+        w3 = load_words(w3_words, H, 0, E, "w3_t", nc.sync)
         w1 += load_words(w1_words, H, 4, 6, "w1_c", nc.sync)
-        w3 += load_words(w3_words, H, 3, 6, "w3_b", nc.sync)
         w2 = load_words(w2_words, N, 0, E, "w2_t", nc.sync)
         load_scales(sc2, w2_scales, nc.sync)
         pos_t = []
@@ -93,7 +88,7 @@ def tile_moe_tk_glu_sigmoid_kernel(
         xw = keep.tile([P, T], U32, align_bytes=64, name="xw")
         for c, (t0, t1) in enumerate(x_cuts):
             xb = keep.tile([P, t1 - t0, 4], BF16, align_bytes=64, name=f"x_bf{c}")
-            (nc.scalar.copy if c == 1 else nc.vector.tensor_copy)(out=xb[:], in_=x_raw[c][:].rearrange("p j t -> p t j"))
+            nc.vector.tensor_copy(out=xb[:], in_=x_raw[c][:].rearrange("p j t -> p t j"))
             cols = slice(t0, t1)
             nc.vector.quantize_mx(
                 out=xw[:, cols].bitcast(FP8X4), scales=xs[:, cols], in_=xb[:].rearrange("p t j -> p (t j)")
@@ -102,7 +97,7 @@ def tile_moe_tk_glu_sigmoid_kernel(
         y_all = keep.tile([P, S], F32, name="y_all")
         gw = []
         gs = []
-        for g, n_tiles in enumerate([1, 1, 2, 2, 2, 2, 2]):
+        for g, n_tiles in enumerate([1] * 8 + [2, 2]):
             n = n_tiles * P
             a = keep.tile([P, n], U32, align_bytes=64, name=f"gw{g}")
             b = keep.tile([P, n], U8, align_bytes=64, name=f"gs{g}")
@@ -142,7 +137,7 @@ def tile_moe_tk_glu_sigmoid_kernel(
             sigs[i] = sig
 
         def b_bank(i):
-            return banks[(1, 3, 1, 4, 5, 7)[i // 2] if i % 2 else (0, 2)[i // 2 % 2]]
+            return banks[(1, 3, 1, 3, 4, 5)[i // 2] if i % 2 else (0, 2)[i // 2 % 2]]
 
         def linear(e):
             for i in (2 * e, 2 * e + 1):
@@ -152,7 +147,7 @@ def tile_moe_tk_glu_sigmoid_kernel(
             h = keep.tile([P, H], BF16, align_bytes=64, name=f"h_bf{i}")
             h_bf[i] = h
             b = b_bank(i)[:].rearrange(read, u=2, d=2)
-            if i < 2:
+            if i < HELPED:
                 lin = keep.tile([P, H], F32, name=f"lin{i}")
                 nc.scalar.copy(lin[:].rearrange(laid, u=2, d=2), b)
                 nc.gpsimd.tensor_tensor(h[:], lin[:], sigs[i][:], MULT)
@@ -162,7 +157,7 @@ def tile_moe_tk_glu_sigmoid_kernel(
         units = [[2 * e, 2 * e + 1] for e in range(E - 1)] + [[2 * E - 2], [2 * E - 1]]
 
         def t_bank(k):
-            return b_bank(units[k][-1]) if k else banks[6]
+            return b_bank(units[k][-1]) if k > 1 else banks[6 + k]
 
         def turn(k):
             tiles = units[k]
@@ -203,41 +198,59 @@ def tile_moe_tk_glu_sigmoid_kernel(
             gating(i)
         linear(0)
         linear(1)
-        gated(0)
-        gated(1)
+        for i in range(HELPED):
+            gated(i)
         gating(8)
         gating(9)
+        gated(3)
         linear(2)
         gating(10)
         gating(11)
-        for e in range(1, E - 1):
+        linear(3)
+        for e in range(2, E - 1):
             gated(2 * e)
             if e + 2 < E:
                 linear(e + 2)
             gated(2 * e + 1)
             turn(e)
-            if e == 2:
-                turn(0)
+            if e < 4:
+                turn(e - 2)
         for k in (E - 1, E):
             gated(units[k][0])
             turn(k)
-        order = [1, 2, 0, 3, 4, 5, 6]
+        order = [2, 0, 3, 1, 4, 5, 6]
         for k in order:
             second(k)
         for k in order:
             fetch(k, nc.vector.tensor_copy if k in ONV else nc.scalar.copy)
 
-        for c, (t0, t1) in enumerate([(0, CUT), (CUT, T)]):
-            n = t1 - t0
+        def weighted(c, t0, t1):
             terms = []
             for r in range(TOP):
-                t = keep.tile([P, n], F32, name=f"term{c}_{r}")
+                t = keep.tile([P, t1 - t0], F32, name=f"term{c}_{r}")
                 nc.vector.tensor_tensor(
                     t[:], y_all[:].indirect(pos_t[r][:, t0 // 16 : t1 // 16]), gate_t[:, r, t0:t1], MULT
                 )
                 terms.append(t)
-            part = keep.tile([P, n], F32, name=f"part{c}")
-            res = keep.tile([P, n], F32, name=f"res{c}")
+            return terms
+
+        terms = weighted(0, 0, CUT)
+        for j in range(CUT // P):
+            cols = slice(j * P, (j + 1) * P)
+            for r in range(TOP):
+                nc.tensor.matmul(
+                    banks[j][:, :P], terms[r][:, cols], ident[:], is_transpose=True, start=r == 0, stop=r == TOP - 1
+                )
+            turned = keep.tile([P, P], F32, name=f"turned{j}")
+            nc.scalar.copy(turned[:], banks[j][:, :P])
+            nc.tensor.transpose(banks[4 + j][:, :P], turned[:], ident[:])
+            res = keep.tile([P, P], F32, name=f"summed{j}")
+            nc.scalar.copy(res[:], banks[4 + j][:, :P])
+            nc.scalar.dma_start(out=out[:, cols], in_=res[:])
+        for c, (t0, t1) in enumerate([(256, 384), (384, 512)]):
+            terms = weighted(c + 1, t0, t1)
+            part = keep.tile([P, t1 - t0], F32, name=f"part{c}")
+            res = keep.tile([P, t1 - t0], F32, name=f"res{c}")
             nc.vector.tensor_tensor(part[:], terms[0][:], terms[1][:], ADD)
             nc.vector.tensor_tensor(res[:], part[:], terms[2][:], ADD)
             nc.sync.dma_start(out=out[:, t0:t1], in_=res[:])

@@ -59,7 +59,7 @@ def tile_moe_tk_glu_sigmoid_kernel(
 
         def load_scales(tile, scales, eng):
             src = scales.bitcast(I32)
-            for q in range(4):
+            for q in (0, 2, 1, 3):
                 eng.dma_start(
                     out=tile[:].bitcast(I32)[32 * q : 32 * q + 4, :].rearrange("p (e c) -> p e c", e=E),
                     in_=src[:, 0, 4 * q : 4 * q + 4, :].rearrange("e q c -> q e c"),
@@ -72,9 +72,10 @@ def tile_moe_tk_glu_sigmoid_kernel(
         w1 = load_words(w1_words, H, 0, 1, "w1_a", nc.sync)
         load_scales(sc1, w1_scales, nc.sync)
         w1 += load_words(w1_words, H, 1, 4, "w1_b", nc.sync)
+        w3 = load_words(w3_words, H, 0, 3, "w3_a", nc.sync)
         load_scales(sc3, w3_scales, nc.sync)
-        w3 = load_words(w3_words, H, 0, E, "w3_t", nc.sync)
         w1 += load_words(w1_words, H, 4, 6, "w1_c", nc.sync)
+        w3 += load_words(w3_words, H, 3, E, "w3_b", nc.sync)
         w2 = load_words(w2_words, N, 0, E, "w2_t", nc.sync)
         load_scales(sc2, w2_scales, nc.sync)
         pos_t = []
@@ -130,14 +131,14 @@ def tile_moe_tk_glu_sigmoid_kernel(
         flats = {}
 
         def gating(i):
-            bank = banks[i if i < 8 else i - 4]
+            bank = banks[i if i < 8 else (4, 5, 1, 2)[i - 8]]
             product(i, w1, sc1, bank)
             sig = keep.tile([P, H], F32, name=f"sig{i}")
             nc.scalar.activation(sig[:].rearrange(laid, u=2, d=2), bank[:].rearrange(read, u=2, d=2), SIGMOID)
             sigs[i] = sig
 
         def b_bank(i):
-            return banks[(1, 3, 1, 3, 4, 5)[i // 2] if i % 2 else (0, 2)[i // 2 % 2]]
+            return banks[(0, 1, 2, 3, 0, 6, 7, 3, 0, 4, 7, 5)[i]]
 
         def linear(e):
             for i in (2 * e, 2 * e + 1):
@@ -157,7 +158,7 @@ def tile_moe_tk_glu_sigmoid_kernel(
         units = [[2 * e, 2 * e + 1] for e in range(E - 1)] + [[2 * E - 2], [2 * E - 1]]
 
         def t_bank(k):
-            return b_bank(units[k][-1]) if k > 1 else banks[6 + k]
+            return b_bank(units[k][-1]) if k > 1 else banks[1 + k]
 
         def turn(k):
             tiles = units[k]

@@ -7,10 +7,14 @@ P = 128
 K, T, E, C, H, N = 512, 512, 6, 256, 512, 128
 S = E * C
 TOP = 3
-HELPED = 3
-CUT = 256
-ONV = (4, 5, 6)
 FLOPS = 2 * S * (2 * K * H + H * N)
+
+BANKS = 8
+X_CUTS = [(0, 256), (256, 384), (384, 512)]
+GATHER_TILES = [1] * BANKS + [2, 2]
+ON_GPSIMD = 3
+Y_ON_VECTOR = 3
+ADDED_IN_PSUM = 256
 
 F32 = mybir.dt.float32
 BF16 = mybir.dt.bfloat16
@@ -31,175 +35,178 @@ def tile_moe_tk_glu_sigmoid_kernel(
     nc = tc.nc
     with ExitStack() as ctx:
         keep = ctx.enter_context(tc.tile_pool(name="keep", bufs=1))
-        work = ctx.enter_context(tc.tile_pool(name="work", bufs=3))
         psum = ctx.enter_context(tc.psum_pool(name="psum", bufs=1))
 
-        sc1 = keep.tile([P, E * H], U8, align_bytes=64, name="sc1")
-        sc3 = keep.tile([P, E * H], U8, align_bytes=64, name="sc3")
-        sc2 = keep.tile([P, E * N], U8, align_bytes=64, name="sc2")
-        xs = keep.tile([P, T], U8, align_bytes=64, name="xs")
-        nc.vector.memset(sc1[:].bitcast(I32), 0)
-        nc.vector.memset(xs[:].bitcast(I32), 0)
-        nc.vector.memset(sc3[:].bitcast(I32), 0)
-        nc.vector.memset(sc2[:].bitcast(I32), 0)
+        w1_plane = keep.tile([P, E * H], U8, align_bytes=64, name="w1_plane")
+        w3_plane = keep.tile([P, E * H], U8, align_bytes=64, name="w3_plane")
+        w2_plane = keep.tile([P, E * N], U8, align_bytes=64, name="w2_plane")
+        x_plane = keep.tile([P, T], U8, align_bytes=64, name="x_plane")
+        for plane in (w1_plane, x_plane, w3_plane, w2_plane):
+            nc.vector.memset(plane[:].bitcast(I32), 0)
 
-        x_view = xT.rearrange("(p j) t -> p j t", j=4)
+        x_rows = xT.rearrange("(p j) t -> p j t", j=4)
         x_raw = []
-        x_cuts = [(0, 256), (256, 384), (384, 512)]
-        for c, (t0, t1) in enumerate(x_cuts):
-            xr = keep.tile([P, 4, t1 - t0], F32, name=f"x_raw{c}")
-            nc.sync.dma_start(out=xr[:], in_=x_view[:, :, t0:t1])
-            x_raw.append(xr)
+        for c, (t0, t1) in enumerate(X_CUTS):
+            raw = keep.tile([P, 4, t1 - t0], F32, name=f"x_raw{c}")
+            nc.sync.dma_start(out=raw[:], in_=x_rows[:, :, t0:t1])
+            x_raw.append(raw)
 
-        def load_words(words, width, e0, e1, name, eng):
-            t = keep.tile([P, (e1 - e0) * 2 * width], U8, align_bytes=64, name=name)
+        def load_words(words, width, e0, e1, name):
+            tile = keep.tile([P, (e1 - e0) * 2 * width], U8, align_bytes=64, name=name)
             src = words.bitcast(I32)[e0:e1, 0].rearrange("e p c -> p e c")
-            eng.dma_start(out=t[:].bitcast(I32).rearrange("p (e c) -> p e c", e=e1 - e0), in_=src)
-            return [t[:, i * 2 * width : (i + 1) * 2 * width] for i in range(e1 - e0)]
+            nc.sync.dma_start(out=tile[:].bitcast(I32).rearrange("p (e c) -> p e c", e=e1 - e0), in_=src)
+            return [tile[:, i * 2 * width : (i + 1) * 2 * width] for i in range(e1 - e0)]
 
-        def load_scales(tile, scales, eng):
-            src = scales.bitcast(I32)
-            for q in (0, 2, 1, 3):
-                eng.dma_start(
-                    out=tile[:].bitcast(I32)[32 * q : 32 * q + 4, :].rearrange("p (e c) -> p e c", e=E),
-                    in_=src[:, 0, 4 * q : 4 * q + 4, :].rearrange("e q c -> q e c"),
-                )
+        def load_plane(plane, scales):
+            rows = scales.bitcast(I32)[:, 0].rearrange("e (quad r) c -> r quad e c", r=4)
+            dst = plane[:].bitcast(I32).rearrange("p (e c) -> p e c", e=E)
+            for r in range(4):
+                nc.sync.dma_start(out=dst[r:P:32], in_=rows[r])
 
         ident = keep.tile([P, P], F32, name="ident")
         make_identity(nc, ident[:])
         offs_t = keep.tile([P, S // 16], U16, name="offs_t")
         nc.sync.dma_start(offs_t[:], offs)
-        w1 = load_words(w1_words, H, 0, 1, "w1_a", nc.sync)
-        load_scales(sc1, w1_scales, nc.sync)
-        w1 += load_words(w1_words, H, 1, 4, "w1_b", nc.sync)
-        w3 = load_words(w3_words, H, 0, 3, "w3_a", nc.sync)
-        load_scales(sc3, w3_scales, nc.sync)
-        w1 += load_words(w1_words, H, 4, 6, "w1_c", nc.sync)
-        w3 += load_words(w3_words, H, 3, E, "w3_b", nc.sync)
-        w2 = load_words(w2_words, N, 0, E, "w2_t", nc.sync)
-        load_scales(sc2, w2_scales, nc.sync)
+        w1 = load_words(w1_words, H, 0, 1, "w1_a")
+        load_plane(w1_plane, w1_scales)
+        w1 += load_words(w1_words, H, 1, 2, "w1_b")
+        w1 += load_words(w1_words, H, 2, 4, "w1_c")
+        w3 = load_words(w3_words, H, 0, 3, "w3_a")
+        load_plane(w3_plane, w3_scales)
+        w1 += load_words(w1_words, H, 4, E, "w1_d")
+        w3 += load_words(w3_words, H, 3, E, "w3_b")
+        w2 = load_words(w2_words, N, 0, E, "w2_t")
+        load_plane(w2_plane, w2_scales)
         pos_t = []
         for r, pos in enumerate((pos1, pos2, pos3)):
-            pt = keep.tile([P, T // 16], U16, name=f"pos_t{r}")
-            nc.sync.dma_start(pt[:], pos)
-            pos_t.append(pt)
+            tile = keep.tile([P, T // 16], U16, name=f"pos_t{r}")
+            nc.sync.dma_start(tile[:], pos)
+            pos_t.append(tile)
         gate_t = keep.tile([P, TOP, T], F32, name="gate_t")
-        nc.sync.dma_start(out=gate_t[:], in_=gate.rearrange("r p t -> p r t"))
+        for r in range(TOP):
+            nc.sync.dma_start(out=gate_t[:, r, :], in_=gate[r])
 
-        xw = keep.tile([P, T], U32, align_bytes=64, name="xw")
-        for c, (t0, t1) in enumerate(x_cuts):
-            xb = keep.tile([P, t1 - t0, 4], BF16, align_bytes=64, name=f"x_bf{c}")
-            nc.vector.tensor_copy(out=xb[:], in_=x_raw[c][:].rearrange("p j t -> p t j"))
-            cols = slice(t0, t1)
+        x_words = keep.tile([P, T], U32, align_bytes=64, name="x_words")
+        for c, (t0, t1) in enumerate(X_CUTS):
+            x_bf = keep.tile([P, t1 - t0, 4], BF16, align_bytes=64, name=f"x_bf{c}")
+            nc.vector.tensor_copy(
+                out=x_bf[:].rearrange("p (g i) j -> p g j i", i=4), in_=x_raw[c][:].rearrange("p j (g i) -> p g j i", i=4)
+            )
             nc.vector.quantize_mx(
-                out=xw[:, cols].bitcast(FP8X4), scales=xs[:, cols], in_=xb[:].rearrange("p t j -> p (t j)")
+                out=x_words[:, t0:t1].bitcast(FP8X4),
+                scales=x_plane[:, t0:t1],
+                in_=x_bf[:].rearrange("p t j -> p (t j)"),
             )
 
         y_all = keep.tile([P, S], F32, name="y_all")
-        gw = []
-        gs = []
-        for g, n_tiles in enumerate([1] * 8 + [2, 2]):
+        slot_words = []
+        slot_plane = []
+        for g, n_tiles in enumerate(GATHER_TILES):
             n = n_tiles * P
-            a = keep.tile([P, n], U32, align_bytes=64, name=f"gw{g}")
-            b = keep.tile([P, n], U8, align_bytes=64, name=f"gs{g}")
-            c0 = len(gw) * P // 16
-            idx = offs_t[:, c0 : c0 + n // 16]
-            nc.vector.tensor_copy(a[:], xw[:].indirect(idx))
-            nc.vector.tensor_copy(b[:], xs[:].indirect(idx))
+            words = keep.tile([P, n], U32, align_bytes=64, name=f"slot_words{g}")
+            plane = keep.tile([P, n], U8, align_bytes=64, name=f"slot_plane{g}")
+            first = len(slot_words) * P // 16
+            entries = offs_t[:, first : first + n // 16]
+            nc.vector.tensor_copy(words[:], x_words[:].indirect(entries))
+            nc.vector.tensor_copy(plane[:], x_plane[:].indirect(entries))
             for i in range(n_tiles):
-                gw.append(a[:, i * P : (i + 1) * P])
-                gs.append(b[:, i * P : (i + 1) * P])
+                slot_words.append(words[:, i * P : (i + 1) * P])
+                slot_plane.append(plane[:, i * P : (i + 1) * P])
 
-        banks = [psum.tile([P, H], F32, name=f"bank{b}") for b in range(8)]
+        banks = [psum.tile([P, H], F32, name=f"bank{n}") for n in range(BANKS)]
+        a_bank = {i: banks[i] for i in range(BANKS)}
+        b_bank = {i: a_bank[i] for i in range(4)}
+        a_bank[8] = a_bank[4]
+        a_bank[9] = a_bank[5]
+        b_bank[5] = a_bank[6]
+        b_bank[6] = a_bank[7]
+        a_bank[10] = b_bank[1]
+        a_bank[11] = b_bank[2]
+        for i in (4, 7, 8, 10):
+            b_bank[i] = b_bank[i - 4]
+        b_bank[9] = a_bank[8]
+        b_bank[11] = a_bank[9]
 
-        def product(i, w, sc, bank):
+        def first_layer(i, words, plane, bank):
             e = i // 2
             nc.tensor.matmul_mx(
                 out=bank[:],
-                lhsT=gw[i].bitcast(FP8X4),
-                lhsT_scale=gs[i],
-                rhs=w[e].bitcast(FP4X4),
-                rhs_scale=sc[:, e * H : (e + 1) * H],
+                lhsT=slot_words[i].bitcast(FP8X4),
+                lhsT_scale=slot_plane[i],
+                rhs=words[e].bitcast(FP4X4),
+                rhs_scale=plane[:, e * H : (e + 1) * H],
                 start=True,
                 stop=True,
             )
 
-        read = "p (m u d) -> p u m d"
-        laid = "p (u m d) -> p u m d"
-        sigs = {}
+        in_psum = "p (m u d) -> p u m d"
+        in_sbuf = "p (u m d) -> p u m d"
+        sig = {}
         h_bf = {}
-        flats = {}
+        h_turned = {}
 
         def gating(i):
-            bank = banks[i if i < 8 else (4, 5, 1, 2)[i - 8]]
-            product(i, w1, sc1, bank)
-            sig = keep.tile([P, H], F32, name=f"sig{i}")
-            nc.scalar.activation(sig[:].rearrange(laid, u=2, d=2), bank[:].rearrange(read, u=2, d=2), SIGMOID)
-            sigs[i] = sig
-
-        def b_bank(i):
-            return banks[(0, 1, 2, 3, 0, 6, 7, 3, 0, 4, 7, 5)[i]]
+            first_layer(i, w1, w1_plane, a_bank[i])
+            sig[i] = keep.tile([P, H], F32, name=f"sig{i}")
+            nc.scalar.activation(sig[i][:].rearrange(in_sbuf, u=2, d=2), a_bank[i][:].rearrange(in_psum, u=2, d=2), SIGMOID)
 
         def linear(e):
             for i in (2 * e, 2 * e + 1):
-                product(i, w3, sc3, b_bank(i))
+                first_layer(i, w3, w3_plane, b_bank[i])
 
         def gated(i):
-            h = keep.tile([P, H], BF16, align_bytes=64, name=f"h_bf{i}")
-            h_bf[i] = h
-            b = b_bank(i)[:].rearrange(read, u=2, d=2)
-            if i < HELPED:
-                lin = keep.tile([P, H], F32, name=f"lin{i}")
-                nc.scalar.copy(lin[:].rearrange(laid, u=2, d=2), b)
-                nc.gpsimd.tensor_tensor(h[:], lin[:], sigs[i][:], MULT)
+            h_bf[i] = keep.tile([P, H], BF16, align_bytes=64, name=f"h_bf{i}")
+            b = b_bank[i][:].rearrange(in_psum, u=2, d=2)
+            if i < ON_GPSIMD:
+                b_sb = keep.tile([P, H], F32, name=f"b_sb{i}")
+                nc.scalar.copy(b_sb[:].rearrange(in_sbuf, u=2, d=2), b)
+                nc.gpsimd.tensor_tensor(h_bf[i][:], b_sb[:], sig[i][:], MULT)
             else:
-                nc.vector.tensor_tensor(h[:].rearrange(laid, u=2, d=2), b, sigs[i][:].rearrange(laid, u=2, d=2), MULT)
+                nc.vector.tensor_tensor(
+                    h_bf[i][:].rearrange(in_sbuf, u=2, d=2), b, sig[i][:].rearrange(in_sbuf, u=2, d=2), MULT
+                )
 
         units = [[2 * e, 2 * e + 1] for e in range(E - 1)] + [[2 * E - 2], [2 * E - 1]]
-
-        def t_bank(k):
-            return b_bank(units[k][-1]) if k > 1 else banks[1 + k]
+        unit_bank = [a_bank[10], a_bank[11]] + [b_bank[tiles[-1]] for tiles in units[2:]]
 
         def turn(k):
-            tiles = units[k]
-            n = len(tiles) * P
-            tp = t_bank(k)[:, : 2 * n].rearrange("p (u r) -> p u r", u=2)
-            for j, i in enumerate(tiles):
-                words = h_bf[i][:].bitcast(F32)
+            n = len(units[k]) * P
+            turned = unit_bank[k][:, : 2 * n].rearrange("p (u s) -> p u s", u=2)
+            for j, i in enumerate(units[k]):
+                pairs = h_bf[i][:].bitcast(F32)
                 for u in range(2):
-                    nc.tensor.transpose(tp[:, u, j * P : (j + 1) * P], words[:, u * P : (u + 1) * P], ident[:])
-            ht = keep.tile([P, n, 4], BF16, align_bytes=64, name=f"ht{k}")
-            flat = ht[:].rearrange("p r d -> p (r d)")
-            nc.scalar.copy(flat.bitcast(F32).rearrange("p (r u) -> p r u", u=2), tp.rearrange("p u r -> p r u"))
-            flats[k] = flat
+                    nc.tensor.transpose(turned[:, u, j * P : (j + 1) * P], pairs[:, u * P : (u + 1) * P], ident[:])
+            tile = keep.tile([P, n, 4], BF16, align_bytes=64, name=f"h_turned{k}")
+            h_turned[k] = tile[:].rearrange("p s t -> p (s t)")
+            nc.scalar.copy(h_turned[k].bitcast(F32).rearrange("p (s u) -> p s u", u=2), turned.rearrange("p u s -> p s u"))
 
-        def second(k):
-            tiles = units[k]
-            n = len(tiles) * P
-            e = tiles[0] // 2
-            hw = keep.tile([P, n], U32, align_bytes=64, name=f"hw{k}")
-            hs = keep.tile([P, n], U8, align_bytes=64, name=f"hs{k}")
-            nc.vector.quantize_mx(out=hw[:].bitcast(FP8X4), scales=hs[:], in_=flats[k])
+        def second_layer(k):
+            n = len(units[k]) * P
+            e = units[k][0] // 2
+            h_words = keep.tile([P, n], U32, align_bytes=64, name=f"h_words{k}")
+            h_plane = keep.tile([P, n], U8, align_bytes=64, name=f"h_plane{k}")
+            nc.vector.quantize_mx(out=h_words[:].bitcast(FP8X4), scales=h_plane[:], in_=h_turned[k])
             nc.tensor.matmul_mx(
-                out=t_bank(k)[:, :n],
+                out=unit_bank[k][:, :n],
                 lhsT=w2[e].bitcast(FP4X4),
-                lhsT_scale=sc2[:, e * N : (e + 1) * N],
-                rhs=hw[:].bitcast(FP8X4),
-                rhs_scale=hs[:],
+                lhsT_scale=w2_plane[:, e * N : (e + 1) * N],
+                rhs=h_words[:].bitcast(FP8X4),
+                rhs_scale=h_plane[:],
                 start=True,
                 stop=True,
             )
 
-        def fetch(k, copy):
-            c0 = units[k][0] * P
+        def fetch_y(k):
+            first = units[k][0] * P
             n = len(units[k]) * P
-            copy(y_all[:, c0 : c0 + n], t_bank(k)[:, :n])
+            copy = nc.vector.tensor_copy if k >= len(units) - Y_ON_VECTOR else nc.scalar.copy
+            copy(y_all[:, first : first + n], unit_bank[k][:, :n])
 
-        for i in range(8):
+        for i in range(BANKS):
             gating(i)
         linear(0)
         linear(1)
-        for i in range(HELPED):
+        for i in range(ON_GPSIMD):
             gated(i)
         gating(8)
         gating(9)
@@ -208,50 +215,54 @@ def tile_moe_tk_glu_sigmoid_kernel(
         gating(10)
         gating(11)
         linear(3)
+        unit_order = []
         for e in range(2, E - 1):
             gated(2 * e)
             if e + 2 < E:
                 linear(e + 2)
             gated(2 * e + 1)
-            turn(e)
-            if e < 4:
-                turn(e - 2)
+            late = [e - 2] if e - 2 < 2 else []
+            for k in [e] + late:
+                turn(k)
+                unit_order.append(k)
         for k in (E - 1, E):
             gated(units[k][0])
             turn(k)
-        order = [2, 0, 3, 1, 4, 5, 6]
-        for k in order:
-            second(k)
-        for k in order:
-            fetch(k, nc.vector.tensor_copy if k in ONV else nc.scalar.copy)
+            unit_order.append(k)
+        for k in unit_order:
+            second_layer(k)
+        for k in unit_order:
+            fetch_y(k)
 
-        def weighted(c, t0, t1):
+        def weighted(t0, t1):
             terms = []
             for r in range(TOP):
-                t = keep.tile([P, t1 - t0], F32, name=f"term{c}_{r}")
+                term = keep.tile([P, t1 - t0], F32, name=f"term{t0}_{r}")
                 nc.vector.tensor_tensor(
-                    t[:], y_all[:].indirect(pos_t[r][:, t0 // 16 : t1 // 16]), gate_t[:, r, t0:t1], MULT
+                    term[:], y_all[:].indirect(pos_t[r][:, t0 // 16 : t1 // 16]), gate_t[:, r, t0:t1], MULT
                 )
-                terms.append(t)
+                terms.append(term)
             return terms
 
-        terms = weighted(0, 0, CUT)
-        for j in range(CUT // P):
+        terms = weighted(0, ADDED_IN_PSUM)
+        for j in range(ADDED_IN_PSUM // P):
             cols = slice(j * P, (j + 1) * P)
+            sum_ps = banks[j][:, :P]
+            back_ps = banks[BANKS // 2 + j][:, :P]
             for r in range(TOP):
-                nc.tensor.matmul(
-                    banks[j][:, :P], terms[r][:, cols], ident[:], is_transpose=True, start=r == 0, stop=r == TOP - 1
-                )
-            turned = keep.tile([P, P], F32, name=f"turned{j}")
-            nc.scalar.copy(turned[:], banks[j][:, :P])
-            nc.tensor.transpose(banks[4 + j][:, :P], turned[:], ident[:])
-            res = keep.tile([P, P], F32, name=f"summed{j}")
-            nc.scalar.copy(res[:], banks[4 + j][:, :P])
-            nc.scalar.dma_start(out=out[:, cols], in_=res[:])
-        for c, (t0, t1) in enumerate([(256, 384), (384, 512)]):
-            terms = weighted(c + 1, t0, t1)
-            part = keep.tile([P, t1 - t0], F32, name=f"part{c}")
-            res = keep.tile([P, t1 - t0], F32, name=f"res{c}")
-            nc.vector.tensor_tensor(part[:], terms[0][:], terms[1][:], ADD)
-            nc.vector.tensor_tensor(res[:], part[:], terms[2][:], ADD)
-            nc.sync.dma_start(out=out[:, t0:t1], in_=res[:])
+                nc.tensor.matmul(sum_ps, terms[r][:, cols], ident[:], is_transpose=True, start=r == 0, stop=r == TOP - 1)
+            by_token = keep.tile([P, P], F32, name=f"by_token{j}")
+            nc.scalar.copy(by_token[:], sum_ps)
+            nc.tensor.transpose(back_ps, by_token[:], ident[:])
+            summed = keep.tile([P, P], F32, name=f"summed{j}")
+            nc.scalar.copy(summed[:], back_ps)
+            nc.scalar.dma_start(out=out[:, cols], in_=summed[:])
+        terms = weighted(ADDED_IN_PSUM, T)
+        blocks = [slice(j * P, (j + 1) * P) for j in range((T - ADDED_IN_PSUM) // P)]
+        part = keep.tile([P, T - ADDED_IN_PSUM], F32, name="part")
+        total = keep.tile([P, T - ADDED_IN_PSUM], F32, name="total")
+        for cols in blocks:
+            nc.vector.tensor_tensor(part[:, cols], terms[0][:, cols], terms[1][:, cols], ADD)
+        for cols in blocks:
+            nc.vector.tensor_tensor(total[:, cols], part[:, cols], terms[2][:, cols], ADD)
+            nc.sync.dma_start(out=out[:, ADDED_IN_PSUM:][:, cols], in_=total[:, cols])

@@ -11,7 +11,7 @@ FLOPS = 2 * S * (2 * K * H + H * N)
 
 BANKS = 8
 X_CUTS = [(0, 256), (256, 384), (384, 512)]
-GATHER_TILES = [1] * BANKS + [2, 2]
+GATHER_TILES = [1, 1, 1, 1, 3, 3, 2]
 ON_GPSIMD = 3
 Y_ON_VECTOR = 3
 ADDED_IN_PSUM = 256
@@ -70,11 +70,12 @@ def tile_moe_tk_glu_sigmoid_kernel(
         w1 = load_words(w1_words, H, 0, 1, "w1_a")
         load_plane(w1_plane, w1_scales)
         w1 += load_words(w1_words, H, 1, 2, "w1_b")
-        w1 += load_words(w1_words, H, 2, 4, "w1_c")
-        w3 = load_words(w3_words, H, 0, 3, "w3_a")
+        w3 = load_words(w3_words, H, 0, 2, "w3_a")
         load_plane(w3_plane, w3_scales)
+        w1 += load_words(w1_words, H, 2, 4, "w1_c")
+        w3 += load_words(w3_words, H, 2, 3, "w3_b")
         w1 += load_words(w1_words, H, 4, E, "w1_d")
-        w3 += load_words(w3_words, H, 3, E, "w3_b")
+        w3 += load_words(w3_words, H, 3, E, "w3_c")
         w2 = load_words(w2_words, N, 0, E, "w2_t")
         load_plane(w2_plane, w2_scales)
         pos_t = []
@@ -83,8 +84,8 @@ def tile_moe_tk_glu_sigmoid_kernel(
             nc.sync.dma_start(tile[:], pos)
             pos_t.append(tile)
         gate_t = keep.tile([P, TOP, T], F32, name="gate_t")
-        for r in range(TOP):
-            nc.sync.dma_start(out=gate_t[:, r, :], in_=gate[r])
+        nc.sync.dma_start(out=gate_t[:, 0, :], in_=gate[0])
+        nc.sync.dma_start(out=gate_t[:, 1:, :], in_=gate[1:].rearrange("r p t -> p r t"))
 
         x_words = keep.tile([P, T], U32, align_bytes=64, name="x_words")
         for c, (t0, t1) in enumerate(X_CUTS):
@@ -98,7 +99,6 @@ def tile_moe_tk_glu_sigmoid_kernel(
                 in_=x_bf[:].rearrange("p t j -> p (t j)"),
             )
 
-        y_all = keep.tile([P, S], F32, name="y_all")
         slot_words = []
         slot_plane = []
         for g, n_tiles in enumerate(GATHER_TILES):
@@ -114,17 +114,13 @@ def tile_moe_tk_glu_sigmoid_kernel(
                 slot_plane.append(plane[:, i * P : (i + 1) * P])
 
         banks = [psum.tile([P, H], F32, name=f"bank{n}") for n in range(BANKS)]
-        a_bank = {i: banks[i] for i in range(BANKS)}
-        b_bank = {i: a_bank[i] for i in range(4)}
-        a_bank[8] = a_bank[4]
-        a_bank[9] = a_bank[5]
-        b_bank[5] = a_bank[6]
-        b_bank[6] = a_bank[7]
-        a_bank[10] = b_bank[1]
-        a_bank[11] = b_bank[2]
-        for i in (4, 7, 8, 10):
-            b_bank[i] = b_bank[i - 4]
-        b_bank[9] = a_bank[8]
+        a_bank = {i: banks[i] for i in range(4)}
+        b_bank = {i: banks[4 + i] for i in range(4)}
+        for i in range(4, 8):
+            b_bank[i] = a_bank[i - 4]
+        for i in range(4, 2 * E):
+            a_bank[i] = b_bank[(i - 4) % ON_GPSIMD]
+        b_bank[8], b_bank[9], b_bank[10] = b_bank[3], b_bank[4], b_bank[5]
         b_bank[11] = a_bank[9]
 
         def first_layer(i, words, plane, bank):
@@ -150,12 +146,12 @@ def tile_moe_tk_glu_sigmoid_kernel(
             sig[i] = keep.tile([P, H], F32, name=f"sig{i}")
             nc.scalar.activation(sig[i][:].rearrange(in_sbuf, u=2, d=2), a_bank[i][:].rearrange(in_psum, u=2, d=2), SIGMOID)
 
-        def linear(e):
-            for i in (2 * e, 2 * e + 1):
+        def linear(*tiles):
+            for i in tiles:
                 first_layer(i, w3, w3_plane, b_bank[i])
 
         def gated(i):
-            h_bf[i] = keep.tile([P, H], BF16, align_bytes=64, name=f"h_bf{i}")
+            h_bf[i] = keep.tile([P, H], BF16, align_bytes=64, name=f"h_bf{i}" if i else "x_plane")
             b = b_bank[i][:].rearrange(in_psum, u=2, d=2)
             if i < ON_GPSIMD:
                 b_sb = keep.tile([P, H], F32, name=f"b_sb{i}")
@@ -167,7 +163,17 @@ def tile_moe_tk_glu_sigmoid_kernel(
                 )
 
         units = [[2 * e, 2 * e + 1] for e in range(E - 1)] + [[2 * E - 2], [2 * E - 1]]
-        unit_bank = [a_bank[10], a_bank[11]] + [b_bank[tiles[-1]] for tiles in units[2:]]
+        unit_bank = [a_bank[10], a_bank[11], b_bank[6]] + [b_bank[tiles[-1]] for tiles in units[3:]]
+        quantised_together = [[2], [3], [0], [1], [4], [5], [6]]
+        fetched_together = [[2, 3], [0, 1], [4], [5], [6]]
+        for group in quantised_together:
+            n = sum(len(units[k]) for k in group) * P
+            tile = keep.tile([P, 4 * n], BF16, align_bytes=64, name=f"h_turned{group[0]}")
+            h_turned[group[0]] = tile[:]
+
+        def place(k, groups):
+            group = [g for g in groups if k in g][0]
+            return group[0], (units[k][0] - units[group[0]][0]) * P
 
         def turn(k):
             n = len(units[k]) * P
@@ -176,63 +182,75 @@ def tile_moe_tk_glu_sigmoid_kernel(
                 pairs = h_bf[i][:].bitcast(F32)
                 for u in range(2):
                     nc.tensor.transpose(turned[:, u, j * P : (j + 1) * P], pairs[:, u * P : (u + 1) * P], ident[:])
-            tile = keep.tile([P, n, 4], BF16, align_bytes=64, name=f"h_turned{k}")
-            h_turned[k] = tile[:].rearrange("p s t -> p (s t)")
-            nc.scalar.copy(h_turned[k].bitcast(F32).rearrange("p (s u) -> p s u", u=2), turned.rearrange("p u s -> p s u"))
+            lead, before = place(k, quantised_together)
+            dst = h_turned[lead][:, 4 * before : 4 * (before + n)]
+            nc.scalar.copy(dst.bitcast(F32).rearrange("p (s u) -> p s u", u=2), turned.rearrange("p u s -> p s u"))
 
-        def second_layer(k):
-            n = len(units[k]) * P
-            e = units[k][0] // 2
-            h_words = keep.tile([P, n], U32, align_bytes=64, name=f"h_words{k}")
-            h_plane = keep.tile([P, n], U8, align_bytes=64, name=f"h_plane{k}")
-            nc.vector.quantize_mx(out=h_words[:].bitcast(FP8X4), scales=h_plane[:], in_=h_turned[k])
-            nc.tensor.matmul_mx(
-                out=unit_bank[k][:, :n],
-                lhsT=w2[e].bitcast(FP4X4),
-                lhsT_scale=w2_plane[:, e * N : (e + 1) * N],
-                rhs=h_words[:].bitcast(FP8X4),
-                rhs_scale=h_plane[:],
-                start=True,
-                stop=True,
-            )
+        def second_layer(group):
+            n_group = sum(len(units[k]) for k in group) * P
+            h_words = keep.tile([P, n_group], U32, align_bytes=64, name=f"h_words{group[0]}")
+            h_plane = keep.tile([P, n_group], U8, align_bytes=64, name=f"h_plane{group[0]}")
+            nc.vector.quantize_mx(out=h_words[:].bitcast(FP8X4), scales=h_plane[:], in_=h_turned[group[0]])
+            for k in group:
+                n = len(units[k]) * P
+                e = units[k][0] // 2
+                first = place(k, quantised_together)[1]
+                lead, before = place(k, fetched_together)
+                nc.tensor.matmul_mx(
+                    out=unit_bank[lead][:, before : before + n],
+                    lhsT=w2[e].bitcast(FP4X4),
+                    lhsT_scale=w2_plane[:, e * N : (e + 1) * N],
+                    rhs=h_words[:, first : first + n].bitcast(FP8X4),
+                    rhs_scale=h_plane[:, first : first + n],
+                    start=True,
+                    stop=True,
+                )
 
-        def fetch_y(k):
-            first = units[k][0] * P
-            n = len(units[k]) * P
-            copy = nc.vector.tensor_copy if k >= len(units) - Y_ON_VECTOR else nc.scalar.copy
-            copy(y_all[:, first : first + n], unit_bank[k][:, :n])
+        def fetch_y(group):
+            first = units[group[0]][0] * P
+            n = sum(len(units[k]) for k in group) * P
+            copy = nc.vector.tensor_copy if group[0] >= E - 2 else nc.scalar.copy
+            copy(y_all[:, first : first + n], unit_bank[group[0]][:, :n])
 
-        for i in range(BANKS):
+        for i in range(4):
             gating(i)
-        linear(0)
-        linear(1)
+        linear(0, 1, 2, 3)
         for i in range(ON_GPSIMD):
             gated(i)
+        gating(4)
+        gating(5)
+        linear(4, 5)
+        gating(6)
+        gating(7)
+        linear(6, 7)
         gating(8)
         gating(9)
         gated(3)
-        linear(2)
+        linear(8)
         gating(10)
+        gated(4)
+        linear(9)
         gating(11)
-        linear(3)
-        unit_order = []
-        for e in range(2, E - 1):
-            gated(2 * e)
-            if e + 2 < E:
-                linear(e + 2)
-            gated(2 * e + 1)
-            late = [e - 2] if e - 2 < 2 else []
-            for k in [e] + late:
-                turn(k)
-                unit_order.append(k)
-        for k in (E - 1, E):
-            gated(units[k][0])
-            turn(k)
-            unit_order.append(k)
-        for k in unit_order:
-            second_layer(k)
-        for k in unit_order:
-            fetch_y(k)
+        gated(5)
+        linear(10, 11)
+        gated(6)
+        turn(2)
+        gated(7)
+        turn(3)
+        turn(0)
+        turn(1)
+        gated(8)
+        gated(9)
+        turn(4)
+        gated(10)
+        turn(5)
+        gated(11)
+        turn(6)
+        y_all = keep.tile([P, S], F32, align_bytes=64, name=f"h_bf{2 * E - 1}")
+        for group in quantised_together:
+            second_layer(group)
+        for group in fetched_together:
+            fetch_y(group)
 
         def weighted(t0, t1):
             terms = []

@@ -10,8 +10,11 @@ TOP = 3
 FLOPS = 2 * S * (2 * K * H + H * N)
 
 BANKS = 8
-X_CUTS = [(0, 256), (256, 384), (384, 512)]
-GATHER_TILES = [1, 1, 1, 1, 3, 3, 2]
+X_LOADS = [(0, 384), (384, 512)]
+X_QUANTISED = [(0, 256), (256, 384), (384, 512)]
+X_CASTS = [(0, 256, False), (256, 384, True), (384, 448, False), (448, 512, True)]
+EARLY = 6
+GATHER_TILES = [1] * EARLY + [3, 3]
 ON_GPSIMD = 3
 Y_ON_VECTOR = 3
 ADDED_IN_PSUM = 256
@@ -46,7 +49,7 @@ def tile_moe_tk_glu_sigmoid_kernel(
 
         x_rows = xT.rearrange("(p j) t -> p j t", j=4)
         x_raw = []
-        for c, (t0, t1) in enumerate(X_CUTS):
+        for c, (t0, t1) in enumerate(X_LOADS):
             raw = keep.tile([P, 4, t1 - t0], F32, name=f"x_raw{c}")
             nc.sync.dma_start(out=raw[:], in_=x_rows[:, :, t0:t1])
             x_raw.append(raw)
@@ -69,10 +72,10 @@ def tile_moe_tk_glu_sigmoid_kernel(
         nc.sync.dma_start(offs_t[:], offs)
         w1 = load_words(w1_words, H, 0, 1, "w1_a")
         load_plane(w1_plane, w1_scales)
-        w1 += load_words(w1_words, H, 1, 2, "w1_b")
+        w1 += load_words(w1_words, H, 1, 3, "w1_b")
         w3 = load_words(w3_words, H, 0, 2, "w3_a")
         load_plane(w3_plane, w3_scales)
-        w1 += load_words(w1_words, H, 2, 4, "w1_c")
+        w1 += load_words(w1_words, H, 3, 4, "w1_c")
         w3 += load_words(w3_words, H, 2, 3, "w3_b")
         w1 += load_words(w1_words, H, 4, E, "w1_d")
         w3 += load_words(w3_words, H, 3, E, "w3_c")
@@ -84,19 +87,21 @@ def tile_moe_tk_glu_sigmoid_kernel(
             nc.sync.dma_start(tile[:], pos)
             pos_t.append(tile)
         gate_t = keep.tile([P, TOP, T], F32, name="gate_t")
-        nc.sync.dma_start(out=gate_t[:, 0, :], in_=gate[0])
-        nc.sync.dma_start(out=gate_t[:, 1:, :], in_=gate[1:].rearrange("r p t -> p r t"))
+        for r in range(TOP):
+            nc.sync.dma_start(out=gate_t[:, r, :], in_=gate[r])
 
         x_words = keep.tile([P, T], U32, align_bytes=64, name="x_words")
-        for c, (t0, t1) in enumerate(X_CUTS):
-            x_bf = keep.tile([P, t1 - t0, 4], BF16, align_bytes=64, name=f"x_bf{c}")
-            nc.vector.tensor_copy(
-                out=x_bf[:].rearrange("p (g i) j -> p g j i", i=4), in_=x_raw[c][:].rearrange("p j (g i) -> p g j i", i=4)
-            )
+        x_bf = [keep.tile([P, t1 - t0, 4], BF16, align_bytes=64, name=f"x_bf{t0}") for t0, t1 in X_QUANTISED]
+        for t0, t1, on_scalar in X_CASTS:
+            src = [x_raw[c][:, :, t0 - a : t1 - a] for c, (a, b) in enumerate(X_LOADS) if a <= t0 < b][0]
+            dst = [x_bf[c][:, t0 - a : t1 - a, :] for c, (a, b) in enumerate(X_QUANTISED) if a <= t0 < b][0]
+            copy = nc.scalar.copy if on_scalar else nc.vector.tensor_copy
+            copy(dst.rearrange("p (g i) j -> p g j i", i=4), src.rearrange("p j (g i) -> p g j i", i=4))
+        for c, (t0, t1) in enumerate(X_QUANTISED):
             nc.vector.quantize_mx(
                 out=x_words[:, t0:t1].bitcast(FP8X4),
                 scales=x_plane[:, t0:t1],
-                in_=x_bf[:].rearrange("p t j -> p (t j)"),
+                in_=x_bf[c][:].rearrange("p t j -> p (t j)"),
             )
 
         slot_words = []
@@ -114,12 +119,12 @@ def tile_moe_tk_glu_sigmoid_kernel(
                 slot_plane.append(plane[:, i * P : (i + 1) * P])
 
         banks = [psum.tile([P, H], F32, name=f"bank{n}") for n in range(BANKS)]
-        a_bank = {i: banks[i] for i in range(4)}
-        b_bank = {i: banks[4 + i] for i in range(4)}
-        for i in range(4, 8):
-            b_bank[i] = a_bank[i - 4]
-        for i in range(4, 2 * E):
-            a_bank[i] = b_bank[(i - 4) % ON_GPSIMD]
+        a_bank = {i: banks[i] for i in range(EARLY)}
+        b_bank = {0: banks[EARLY], 1: banks[EARLY + 1]}
+        for i in range(2, 8):
+            b_bank[i] = a_bank[i - 2]
+        for i in range(EARLY, 2 * E):
+            a_bank[i] = b_bank[i % ON_GPSIMD]
         b_bank[8], b_bank[9], b_bank[10] = b_bank[3], b_bank[4], b_bank[5]
         b_bank[11] = a_bank[9]
 
@@ -212,18 +217,16 @@ def tile_moe_tk_glu_sigmoid_kernel(
             copy = nc.vector.tensor_copy if group[0] >= E - 2 else nc.scalar.copy
             copy(y_all[:, first : first + n], unit_bank[group[0]][:, :n])
 
-        for i in range(4):
+        for i in range(EARLY):
             gating(i)
         linear(0, 1, 2, 3)
         for i in range(ON_GPSIMD):
             gated(i)
-        gating(4)
-        gating(5)
-        linear(4, 5)
         gating(6)
+        linear(4, 5)
         gating(7)
-        linear(6, 7)
         gating(8)
+        linear(6, 7)
         gating(9)
         gated(3)
         linear(8)

@@ -60,10 +60,10 @@ def tile_moe_tk_glu_sigmoid_kernel(
             nc.sync.dma_start(out=tile[:].bitcast(I32).rearrange("p (e c) -> p e c", e=e1 - e0), in_=src)
             return [tile[:, i * 2 * width : (i + 1) * 2 * width] for i in range(e1 - e0)]
 
-        def load_plane(plane, scales):
+        def load_plane(plane, scales, which=range(4)):
             rows = scales.bitcast(I32)[:, 0].rearrange("e (quad r) c -> r quad e c", r=4)
             dst = plane[:].bitcast(I32).rearrange("p (e c) -> p e c", e=E)
-            for r in range(4):
+            for r in which:
                 nc.sync.dma_start(out=dst[r:P:32], in_=rows[r])
 
         ident = keep.tile([P, P], F32, name="ident")
@@ -72,13 +72,14 @@ def tile_moe_tk_glu_sigmoid_kernel(
         nc.sync.dma_start(offs_t[:], offs)
         w1 = load_words(w1_words, H, 0, 1, "w1_a")
         load_plane(w1_plane, w1_scales)
+        load_plane(w3_plane, w3_scales, [0])
         w1 += load_words(w1_words, H, 1, 3, "w1_b")
-        w3 = load_words(w3_words, H, 0, 2, "w3_a")
-        load_plane(w3_plane, w3_scales)
+        load_plane(w3_plane, w3_scales, [1])
+        w3 = load_words(w3_words, H, 0, 4, "w3_a")
+        load_plane(w3_plane, w3_scales, [2, 3])
         w1 += load_words(w1_words, H, 3, 4, "w1_c")
-        w3 += load_words(w3_words, H, 2, 3, "w3_b")
         w1 += load_words(w1_words, H, 4, E, "w1_d")
-        w3 += load_words(w3_words, H, 3, E, "w3_c")
+        w3 += load_words(w3_words, H, 4, E, "w3_c")
         w2 = load_words(w2_words, N, 0, E, "w2_t")
         load_plane(w2_plane, w2_scales)
         pos_t = []
@@ -95,8 +96,10 @@ def tile_moe_tk_glu_sigmoid_kernel(
         for t0, t1, on_scalar in X_CASTS:
             src = [x_raw[c][:, :, t0 - a : t1 - a] for c, (a, b) in enumerate(X_LOADS) if a <= t0 < b][0]
             dst = [x_bf[c][:, t0 - a : t1 - a, :] for c, (a, b) in enumerate(X_QUANTISED) if a <= t0 < b][0]
-            copy = nc.scalar.copy if on_scalar else nc.vector.tensor_copy
-            copy(dst.rearrange("p (g i) j -> p g j i", i=4), src.rearrange("p j (g i) -> p g j i", i=4))
+            if on_scalar:
+                nc.scalar.copy(dst, src.rearrange("p j t -> p t j"))
+            else:
+                nc.vector.tensor_copy(dst.rearrange("p (g i) j -> p g j i", i=4), src.rearrange("p j (g i) -> p g j i", i=4))
         for c, (t0, t1) in enumerate(X_QUANTISED):
             nc.vector.quantize_mx(
                 out=x_words[:, t0:t1].bitcast(FP8X4),
@@ -219,14 +222,14 @@ def tile_moe_tk_glu_sigmoid_kernel(
 
         for i in range(EARLY):
             gating(i)
-        linear(0, 1, 2, 3)
+        linear(*range(EARLY))
         for i in range(ON_GPSIMD):
             gated(i)
         gating(6)
-        linear(4, 5)
+        linear(6)
         gating(7)
+        linear(7)
         gating(8)
-        linear(6, 7)
         gating(9)
         gated(3)
         linear(8)

@@ -159,7 +159,7 @@ def tile_moe_tk_glu_sigmoid_kernel(
                 first_layer(i, w3, w3_plane, b_bank[i])
 
         def gated(i):
-            h_bf[i] = keep.tile([P, H], BF16, align_bytes=64, name=f"h_bf{i}" if i else "x_plane")
+            h_bf[i] = keep.tile([P, H], BF16, align_bytes=64, name=f"h_bf{i}")
             b = b_bank[i][:].rearrange(in_psum, u=2, d=2)
             if i < ON_GPSIMD:
                 b_sb = keep.tile([P, H], F32, name=f"b_sb{i}")

@@ -16,8 +16,8 @@ X_CASTS = [(0, 256, False), (256, 384, True), (384, 448, False), (448, 512, True
 EARLY = 6
 GATHER_TILES = [1] * EARLY + [3, 3]
 ON_GPSIMD = 3
-Y_ON_VECTOR = 3
 ADDED_IN_PSUM = 256
+SECOND_ON_SCALAR = 128
 
 F32 = mybir.dt.float32
 BF16 = mybir.dt.bfloat16
@@ -28,6 +28,7 @@ U8 = mybir.dt.uint8
 FP8X4 = mybir.dt.float8_e4m3fn_x4
 FP4X4 = mybir.dt.float4_e2m1fn_x4
 SIGMOID = mybir.ActivationFunctionType.Sigmoid
+COPY = mybir.ActivationFunctionType.Copy
 MULT = mybir.AluOpType.mult
 ADD = mybir.AluOpType.add
 
@@ -258,35 +259,47 @@ def tile_moe_tk_glu_sigmoid_kernel(
         for group in fetched_together:
             fetch_y(group)
 
-        def weighted(t0, t1):
-            terms = []
-            for r in range(TOP):
-                term = keep.tile([P, t1 - t0], F32, name=f"term{t0}_{r}")
-                nc.vector.tensor_tensor(
-                    term[:], y_all[:].indirect(pos_t[r][:, t0 // 16 : t1 // 16]), gate_t[:, r, t0:t1], MULT
-                )
-                terms.append(term)
-            return terms
+        def looked_up(r, t0, t1):
+            return y_all[:].indirect(pos_t[r][:, t0 // 16 : t1 // 16])
 
-        terms = weighted(0, ADDED_IN_PSUM)
-        for j in range(ADDED_IN_PSUM // P):
-            cols = slice(j * P, (j + 1) * P)
-            sum_ps = banks[j][:, :P]
-            back_ps = banks[BANKS // 2 + j][:, :P]
-            for r in range(TOP):
-                nc.tensor.matmul(sum_ps, terms[r][:, cols], ident[:], is_transpose=True, start=r == 0, stop=r == TOP - 1)
-            by_token = keep.tile([P, P], F32, name=f"by_token{j}")
-            nc.scalar.copy(by_token[:], sum_ps)
-            nc.tensor.transpose(back_ps, by_token[:], ident[:])
-            summed = keep.tile([P, P], F32, name=f"summed{j}")
-            nc.scalar.copy(summed[:], back_ps)
-            nc.scalar.dma_start(out=out[:, cols], in_=summed[:])
-        terms = weighted(ADDED_IN_PSUM, T)
+        def fetch(r, t0, t1):
+            tile = keep.tile([P, t1 - t0], F32, name=f"fetched{r}_{t0}")
+            nc.scalar.activation(tile[:], looked_up(r, t0, t1), COPY)
+            return tile[:]
+
+        def weigh(term, values, r, t0, t1):
+            nc.vector.tensor_tensor(term, values, gate_t[:, r, t0:t1], MULT)
+
+        split = T - SECOND_ON_SCALAR
+        third = [fetch(2, 0, ADDED_IN_PSUM), fetch(2, ADDED_IN_PSUM, T)]
+        second = fetch(1, split, T)
+        early = [keep.tile([P, ADDED_IN_PSUM], F32, name=f"early{r}") for r in range(TOP)]
+        late = [keep.tile([P, T - ADDED_IN_PSUM], F32, name=f"late{r}") for r in range(TOP)]
+        weigh(early[0][:], looked_up(0, 0, ADDED_IN_PSUM), 0, 0, ADDED_IN_PSUM)
+        weigh(early[1][:], looked_up(1, 0, ADDED_IN_PSUM), 1, 0, ADDED_IN_PSUM)
+        weigh(early[2][:], third[0], 2, 0, ADDED_IN_PSUM)
+        weigh(late[0][:], looked_up(0, ADDED_IN_PSUM, T), 0, ADDED_IN_PSUM, T)
+        weigh(late[1][:, : split - ADDED_IN_PSUM], looked_up(1, ADDED_IN_PSUM, split), 1, ADDED_IN_PSUM, split)
+        weigh(late[2][:], third[1], 2, ADDED_IN_PSUM, T)
+        weigh(late[1][:, split - ADDED_IN_PSUM :], second, 1, split, T)
+
+        blocks = [slice(j * P, (j + 1) * P) for j in range(ADDED_IN_PSUM // P)]
+        for r in range(TOP):
+            for j, cols in enumerate(blocks):
+                nc.tensor.matmul(banks[j][:, :P], early[r][:, cols], ident[:], is_transpose=True, start=r == 0, stop=r == TOP - 1)
+        by_token = keep.tile([P, ADDED_IN_PSUM], F32, name="by_token")
+        summed = keep.tile([P, ADDED_IN_PSUM], F32, name="summed")
+        for j, cols in enumerate(blocks):
+            nc.scalar.copy(by_token[:, cols], banks[j][:, :P])
+            nc.tensor.transpose(banks[BANKS // 2 + j][:, :P], by_token[:, cols], ident[:])
+        for j, cols in enumerate(blocks):
+            nc.scalar.copy(summed[:, cols], banks[BANKS // 2 + j][:, :P])
+            nc.scalar.dma_start(out=out[:, cols], in_=summed[:, cols])
         blocks = [slice(j * P, (j + 1) * P) for j in range((T - ADDED_IN_PSUM) // P)]
         part = keep.tile([P, T - ADDED_IN_PSUM], F32, name="part")
         total = keep.tile([P, T - ADDED_IN_PSUM], F32, name="total")
         for cols in blocks:
-            nc.vector.tensor_tensor(part[:, cols], terms[0][:, cols], terms[1][:, cols], ADD)
+            nc.vector.tensor_tensor(part[:, cols], late[0][:, cols], late[2][:, cols], ADD)
         for cols in blocks:
-            nc.vector.tensor_tensor(total[:, cols], part[:, cols], terms[2][:, cols], ADD)
+            nc.vector.tensor_tensor(total[:, cols], part[:, cols], late[1][:, cols], ADD)
             nc.sync.dma_start(out=out[:, ADDED_IN_PSUM:][:, cols], in_=total[:, cols])

@@ -17,7 +17,7 @@ EARLY = 6
 GATHER_TILES = [1] * EARLY + [3, 3]
 ON_GPSIMD = 3
 ADDED_IN_PSUM = 256
-SECOND_ON_SCALAR = 128
+SECOND_ON_SCALAR = 256
 
 F32 = mybir.dt.float32
 BF16 = mybir.dt.bfloat16
@@ -279,7 +279,6 @@ def tile_moe_tk_glu_sigmoid_kernel(
         weigh(early[1][:], looked_up(1, 0, ADDED_IN_PSUM), 1, 0, ADDED_IN_PSUM)
         weigh(early[2][:], third[0], 2, 0, ADDED_IN_PSUM)
         weigh(late[0][:], looked_up(0, ADDED_IN_PSUM, T), 0, ADDED_IN_PSUM, T)
-        weigh(late[1][:, : split - ADDED_IN_PSUM], looked_up(1, ADDED_IN_PSUM, split), 1, ADDED_IN_PSUM, split)
         weigh(late[2][:], third[1], 2, ADDED_IN_PSUM, T)
         weigh(late[1][:, split - ADDED_IN_PSUM :], second, 1, split, T)
 

@@ -11,8 +11,7 @@ FLOPS = 2 * S * (2 * K * H + H * N)
 
 BANKS = 8
 X_LOADS = [(0, 384), (384, 512)]
-X_QUANTISED = [(0, 256), (256, 384), (384, 512)]
-X_CASTS = [(0, 256, False), (256, 384, True), (384, 448, False), (448, 512, True)]
+X_QUANTISED = [(0, 128), (128, 384), (384, 512)]
 EARLY = 6
 GATHER_TILES = [1] * EARLY + [3, 3]
 ON_GPSIMD = 3
@@ -94,19 +93,31 @@ def tile_moe_tk_glu_sigmoid_kernel(
 
         x_words = keep.tile([P, T], U32, align_bytes=64, name="x_words")
         x_bf = [keep.tile([P, t1 - t0, 4], BF16, align_bytes=64, name=f"x_bf{t0}") for t0, t1 in X_QUANTISED]
-        for t0, t1, on_scalar in X_CASTS:
+
+        def cast(t0, t1, on_scalar):
             src = [x_raw[c][:, :, t0 - a : t1 - a] for c, (a, b) in enumerate(X_LOADS) if a <= t0 < b][0]
             dst = [x_bf[c][:, t0 - a : t1 - a, :] for c, (a, b) in enumerate(X_QUANTISED) if a <= t0 < b][0]
             if on_scalar:
                 nc.scalar.copy(dst, src.rearrange("p j t -> p t j"))
             else:
                 nc.vector.tensor_copy(dst.rearrange("p (g i) j -> p g j i", i=4), src.rearrange("p j (g i) -> p g j i", i=4))
-        for c, (t0, t1) in enumerate(X_QUANTISED):
+
+        def quantise(c):
+            t0, t1 = X_QUANTISED[c]
             nc.vector.quantize_mx(
                 out=x_words[:, t0:t1].bitcast(FP8X4),
                 scales=x_plane[:, t0:t1],
                 in_=x_bf[c][:].rearrange("p t j -> p (t j)"),
             )
+
+        cast(256, 384, True)
+        cast(0, 128, False)
+        cast(128, 256, False)
+        quantise(0)
+        cast(448, 512, True)
+        cast(384, 448, False)
+        quantise(1)
+        quantise(2)
 
         slot_words = []
         slot_plane = []

from contextlib import ExitStack

import concourse.mybir as mybir
from concourse.masks import make_identity

P = 128
K, T, E, C, H, N = 512, 512, 6, 256, 512, 128
S = E * C
TOP = 3
FLOPS = 2 * S * (2 * K * H + H * N)

BANKS = 8
X_LOADS = [(0, 384), (384, 512)]
X_QUANTISED = [(0, 128), (128, 384), (384, 512)]
EARLY = 6
GATHER_TILES = [1] * EARLY + [3, 3]
ON_GPSIMD = 3
ADDED_IN_PSUM = 256
SECOND_ON_SCALAR = 256

F32 = mybir.dt.float32
BF16 = mybir.dt.bfloat16
I32 = mybir.dt.int32
U32 = mybir.dt.uint32
U16 = mybir.dt.uint16
U8 = mybir.dt.uint8
FP8X4 = mybir.dt.float8_e4m3fn_x4
FP4X4 = mybir.dt.float4_e2m1fn_x4
SIGMOID = mybir.ActivationFunctionType.Sigmoid
COPY = mybir.ActivationFunctionType.Copy
MULT = mybir.AluOpType.mult
ADD = mybir.AluOpType.add


def tile_moe_tk_glu_sigmoid_kernel(
    tc, xT, w1_words, w1_scales, w3_words, w3_scales, w2_words, w2_scales, gate, offs, pos1, pos2, pos3, out
):
    nc = tc.nc
    with ExitStack() as ctx:
        keep = ctx.enter_context(tc.tile_pool(name="keep", bufs=1))
        psum = ctx.enter_context(tc.psum_pool(name="psum", bufs=1))

        w1_plane = keep.tile([P, E * H], U8, align_bytes=64, name="w1_plane")
        w3_plane = keep.tile([P, E * H], U8, align_bytes=64, name="w3_plane")
        w2_plane = keep.tile([P, E * N], U8, align_bytes=64, name="w2_plane")
        x_plane = keep.tile([P, T], U8, align_bytes=64, name="x_plane")
        for plane in (w1_plane, x_plane, w3_plane, w2_plane):
            nc.vector.memset(plane[:].bitcast(I32), 0)

        x_rows = xT.rearrange("(p j) t -> p j t", j=4)
        x_raw = []
        for c, (t0, t1) in enumerate(X_LOADS):
            raw = keep.tile([P, 4, t1 - t0], F32, name=f"x_raw{c}")
            nc.sync.dma_start(out=raw[:], in_=x_rows[:, :, t0:t1])
            x_raw.append(raw)

        def load_words(words, width, e0, e1, name):
            tile = keep.tile([P, (e1 - e0) * 2 * width], U8, align_bytes=64, name=name)
            src = words.bitcast(I32)[e0:e1, 0].rearrange("e p c -> p e c")
            nc.sync.dma_start(out=tile[:].bitcast(I32).rearrange("p (e c) -> p e c", e=e1 - e0), in_=src)
            return [tile[:, i * 2 * width : (i + 1) * 2 * width] for i in range(e1 - e0)]

        def load_plane(plane, scales, which=range(4)):
            rows = scales.bitcast(I32)[:, 0].rearrange("e (quad r) c -> r quad e c", r=4)
            dst = plane[:].bitcast(I32).rearrange("p (e c) -> p e c", e=E)
            for r in which:
                nc.sync.dma_start(out=dst[r:P:32], in_=rows[r])

        ident = keep.tile([P, P], F32, name="ident")
        make_identity(nc, ident[:])
        offs_t = keep.tile([P, S // 16], U16, name="offs_t")
        nc.sync.dma_start(offs_t[:], offs)
        w1 = load_words(w1_words, H, 0, 1, "w1_a")
        load_plane(w1_plane, w1_scales)
        load_plane(w3_plane, w3_scales, [0])
        w1 += load_words(w1_words, H, 1, 3, "w1_b")
        load_plane(w3_plane, w3_scales, [1])
        w3 = load_words(w3_words, H, 0, 4, "w3_a")
        load_plane(w3_plane, w3_scales, [2, 3])
        w1 += load_words(w1_words, H, 3, 4, "w1_c")
        w1 += load_words(w1_words, H, 4, E, "w1_d")
        w3 += load_words(w3_words, H, 4, E, "w3_c")
        w2 = load_words(w2_words, N, 0, E, "w2_t")
        load_plane(w2_plane, w2_scales)
        pos_t = []
        for r, pos in enumerate((pos1, pos2, pos3)):
            tile = keep.tile([P, T // 16], U16, name=f"pos_t{r}")
            nc.sync.dma_start(tile[:], pos)
            pos_t.append(tile)
        gate_t = keep.tile([P, TOP, T], F32, name="gate_t")
        for r in range(TOP):
            nc.sync.dma_start(out=gate_t[:, r, :], in_=gate[r])

        x_words = keep.tile([P, T], U32, align_bytes=64, name="x_words")
        x_bf = [keep.tile([P, t1 - t0, 4], BF16, align_bytes=64, name=f"x_bf{t0}") for t0, t1 in X_QUANTISED]

        def cast(t0, t1, on_scalar):
            src = [x_raw[c][:, :, t0 - a : t1 - a] for c, (a, b) in enumerate(X_LOADS) if a <= t0 < b][0]
            dst = [x_bf[c][:, t0 - a : t1 - a, :] for c, (a, b) in enumerate(X_QUANTISED) if a <= t0 < b][0]
            if on_scalar:
                nc.scalar.copy(dst, src.rearrange("p j t -> p t j"))
            else:
                nc.vector.tensor_copy(dst.rearrange("p (g i) j -> p g j i", i=4), src.rearrange("p j (g i) -> p g j i", i=4))

        def quantise(c):
            t0, t1 = X_QUANTISED[c]
            nc.vector.quantize_mx(
                out=x_words[:, t0:t1].bitcast(FP8X4),
                scales=x_plane[:, t0:t1],
                in_=x_bf[c][:].rearrange("p t j -> p (t j)"),
            )

        cast(256, 384, True)
        cast(0, 128, False)
        cast(128, 256, False)
        quantise(0)
        cast(448, 512, True)
        cast(384, 448, False)
        quantise(1)
        quantise(2)

        slot_words = []
        slot_plane = []
        for g, n_tiles in enumerate(GATHER_TILES):
            n = n_tiles * P
            words = keep.tile([P, n], U32, align_bytes=64, name=f"slot_words{g}")
            plane = keep.tile([P, n], U8, align_bytes=64, name=f"slot_plane{g}")
            first = len(slot_words) * P // 16
            entries = offs_t[:, first : first + n // 16]
            nc.vector.tensor_copy(words[:], x_words[:].indirect(entries))
            nc.vector.tensor_copy(plane[:], x_plane[:].indirect(entries))
            for i in range(n_tiles):
                slot_words.append(words[:, i * P : (i + 1) * P])
                slot_plane.append(plane[:, i * P : (i + 1) * P])

        banks = [psum.tile([P, H], F32, name=f"bank{n}") for n in range(BANKS)]
        a_bank = {i: banks[i] for i in range(EARLY)}
        b_bank = {0: banks[EARLY], 1: banks[EARLY + 1]}
        for i in range(2, 8):
            b_bank[i] = a_bank[i - 2]
        for i in range(EARLY, 2 * E):
            a_bank[i] = b_bank[i % ON_GPSIMD]
        b_bank[8], b_bank[9], b_bank[10] = b_bank[3], b_bank[4], b_bank[5]
        b_bank[11] = a_bank[9]

        def first_layer(i, words, plane, bank):
            e = i // 2
            nc.tensor.matmul_mx(
                out=bank[:],
                lhsT=slot_words[i].bitcast(FP8X4),
                lhsT_scale=slot_plane[i],
                rhs=words[e].bitcast(FP4X4),
                rhs_scale=plane[:, e * H : (e + 1) * H],
                start=True,
                stop=True,
            )

        in_psum = "p (m u d) -> p u m d"
        in_sbuf = "p (u m d) -> p u m d"
        sig = {}
        h_bf = {}
        h_turned = {}

        def gating(i):
            first_layer(i, w1, w1_plane, a_bank[i])
            sig[i] = keep.tile([P, H], F32, name=f"sig{i}")
            nc.scalar.activation(sig[i][:].rearrange(in_sbuf, u=2, d=2), a_bank[i][:].rearrange(in_psum, u=2, d=2), SIGMOID)

        def linear(*tiles):
            for i in tiles:
                first_layer(i, w3, w3_plane, b_bank[i])

        def gated(i):
            h_bf[i] = keep.tile([P, H], BF16, align_bytes=64, name=f"h_bf{i}")
            b = b_bank[i][:].rearrange(in_psum, u=2, d=2)
            if i < ON_GPSIMD:
                b_sb = keep.tile([P, H], F32, name=f"b_sb{i}")
                nc.scalar.copy(b_sb[:].rearrange(in_sbuf, u=2, d=2), b)
                nc.gpsimd.tensor_tensor(h_bf[i][:], b_sb[:], sig[i][:], MULT)
            else:
                nc.vector.tensor_tensor(
                    h_bf[i][:].rearrange(in_sbuf, u=2, d=2), b, sig[i][:].rearrange(in_sbuf, u=2, d=2), MULT
                )

        units = [[2 * e, 2 * e + 1] for e in range(E - 1)] + [[2 * E - 2], [2 * E - 1]]
        unit_bank = [a_bank[10], a_bank[11], b_bank[6]] + [b_bank[tiles[-1]] for tiles in units[3:]]
        quantised_together = [[2], [3], [0], [1], [4], [5], [6]]
        fetched_together = [[2, 3], [0, 1], [4], [5], [6]]
        for group in quantised_together:
            n = sum(len(units[k]) for k in group) * P
            tile = keep.tile([P, 4 * n], BF16, align_bytes=64, name=f"h_turned{group[0]}")
            h_turned[group[0]] = tile[:]

        def place(k, groups):
            group = [g for g in groups if k in g][0]
            return group[0], (units[k][0] - units[group[0]][0]) * P

        def turn(k):
            n = len(units[k]) * P
            turned = unit_bank[k][:, : 2 * n].rearrange("p (u s) -> p u s", u=2)
            for j, i in enumerate(units[k]):
                pairs = h_bf[i][:].bitcast(F32)
                for u in range(2):
                    nc.tensor.transpose(turned[:, u, j * P : (j + 1) * P], pairs[:, u * P : (u + 1) * P], ident[:])
            lead, before = place(k, quantised_together)
            dst = h_turned[lead][:, 4 * before : 4 * (before + n)]
            nc.scalar.copy(dst.bitcast(F32).rearrange("p (s u) -> p s u", u=2), turned.rearrange("p u s -> p s u"))

        def second_layer(group):
            n_group = sum(len(units[k]) for k in group) * P
            h_words = keep.tile([P, n_group], U32, align_bytes=64, name=f"h_words{group[0]}")
            h_plane = keep.tile([P, n_group], U8, align_bytes=64, name=f"h_plane{group[0]}")
            nc.vector.quantize_mx(out=h_words[:].bitcast(FP8X4), scales=h_plane[:], in_=h_turned[group[0]])
            for k in group:
                n = len(units[k]) * P
                e = units[k][0] // 2
                first = place(k, quantised_together)[1]
                lead, before = place(k, fetched_together)
                nc.tensor.matmul_mx(
                    out=unit_bank[lead][:, before : before + n],
                    lhsT=w2[e].bitcast(FP4X4),
                    lhsT_scale=w2_plane[:, e * N : (e + 1) * N],
                    rhs=h_words[:, first : first + n].bitcast(FP8X4),
                    rhs_scale=h_plane[:, first : first + n],
                    start=True,
                    stop=True,
                )

        def fetch_y(group):
            first = units[group[0]][0] * P
            n = sum(len(units[k]) for k in group) * P
            copy = nc.vector.tensor_copy if group[0] >= E - 2 else nc.scalar.copy
            copy(y_all[:, first : first + n], unit_bank[group[0]][:, :n])

        for i in range(EARLY):
            gating(i)
        linear(*range(EARLY))
        for i in range(ON_GPSIMD):
            gated(i)
        gating(6)
        linear(6)
        gating(7)
        linear(7)
        gating(8)
        gating(9)
        gated(3)
        linear(8)
        gating(10)
        gated(4)
        linear(9)
        gating(11)
        gated(5)
        linear(10, 11)
        gated(6)
        turn(2)
        gated(7)
        turn(3)
        turn(0)
        turn(1)
        gated(8)
        gated(9)
        turn(4)
        gated(10)
        turn(5)
        gated(11)
        turn(6)
        y_all = keep.tile([P, S], F32, align_bytes=64, name=f"h_bf{2 * E - 1}")
        for group in quantised_together:
            second_layer(group)
        for group in fetched_together:
            fetch_y(group)

        def looked_up(r, t0, t1):
            return y_all[:].indirect(pos_t[r][:, t0 // 16 : t1 // 16])

        def fetch(r, t0, t1):
            tile = keep.tile([P, t1 - t0], F32, name=f"fetched{r}_{t0}")
            nc.scalar.activation(tile[:], looked_up(r, t0, t1), COPY)
            return tile[:]

        def weigh(term, values, r, t0, t1):
            nc.vector.tensor_tensor(term, values, gate_t[:, r, t0:t1], MULT)

        split = T - SECOND_ON_SCALAR
        third = [fetch(2, 0, ADDED_IN_PSUM), fetch(2, ADDED_IN_PSUM, T)]
        second = fetch(1, split, T)
        early = [keep.tile([P, ADDED_IN_PSUM], F32, name=f"early{r}") for r in range(TOP)]
        late = [keep.tile([P, T - ADDED_IN_PSUM], F32, name=f"late{r}") for r in range(TOP)]
        weigh(early[0][:], looked_up(0, 0, ADDED_IN_PSUM), 0, 0, ADDED_IN_PSUM)
        weigh(early[1][:], looked_up(1, 0, ADDED_IN_PSUM), 1, 0, ADDED_IN_PSUM)
        weigh(early[2][:], third[0], 2, 0, ADDED_IN_PSUM)
        weigh(late[0][:], looked_up(0, ADDED_IN_PSUM, T), 0, ADDED_IN_PSUM, T)
        weigh(late[2][:], third[1], 2, ADDED_IN_PSUM, T)
        weigh(late[1][:, split - ADDED_IN_PSUM :], second, 1, split, T)

        blocks = [slice(j * P, (j + 1) * P) for j in range(ADDED_IN_PSUM // P)]
        for r in range(TOP):
            for j, cols in enumerate(blocks):
                nc.tensor.matmul(banks[j][:, :P], early[r][:, cols], ident[:], is_transpose=True, start=r == 0, stop=r == TOP - 1)
        by_token = keep.tile([P, ADDED_IN_PSUM], F32, name="by_token")
        summed = keep.tile([P, ADDED_IN_PSUM], F32, name="summed")
        for j, cols in enumerate(blocks):
            nc.scalar.copy(by_token[:, cols], banks[j][:, :P])
            nc.tensor.transpose(banks[BANKS // 2 + j][:, :P], by_token[:, cols], ident[:])
        for j, cols in enumerate(blocks):
            nc.scalar.copy(summed[:, cols], banks[BANKS // 2 + j][:, :P])
            nc.scalar.dma_start(out=out[:, cols], in_=summed[:, cols])
        blocks = [slice(j * P, (j + 1) * P) for j in range((T - ADDED_IN_PSUM) // P)]
        part = keep.tile([P, T - ADDED_IN_PSUM], F32, name="part")
        total = keep.tile([P, T - ADDED_IN_PSUM], F32, name="total")
        for cols in blocks:
            nc.vector.tensor_tensor(part[:, cols], late[0][:, cols], late[2][:, cols], ADD)
        for cols in blocks:
            nc.vector.tensor_tensor(total[:, cols], part[:, cols], late[1][:, cols], ADD)
            nc.sync.dma_start(out=out[:, ADDED_IN_PSUM:][:, cols], in_=total[:, cols])
